import numpy as np
import ml_dtypes


def mxq(x, axis, fmt="e4m3"):
    dtype, down = {"e4m3": (ml_dtypes.float8_e4m3fn, 7), "e5m2": (ml_dtypes.float8_e5m2, 14)}[fmt]
    v = np.moveaxis(np.asarray(x, np.float32).astype(ml_dtypes.bfloat16).astype(np.float64), axis, -1)
    blocks = v.reshape(v.shape[:-1] + (-1, 32))
    amax = np.abs(blocks).max(-1, keepdims=True)
    byte = np.maximum(np.where(amax > 0, np.frexp(amax)[1] - 1 + 127, 0) - down, 1)
    scale = np.exp2(byte - 127.0)
    codes = (blocks / scale).astype(np.float32).astype(dtype).astype(np.float64)
    return np.moveaxis((codes * scale).reshape(v.shape), -1, axis)


WIDE = False


def mx_kscale(k):
    if not WIDE:
        return np.ones(k)
    levels = np.array([10, -10, 5, -5, 0])
    if k % 512:
        return np.exp2(np.random.permutation(np.resize(levels, k // 32))).repeat(32)
    a = np.empty((k // 512, 16))
    for p in range(k // 512):
        a[p, :8] = np.random.permutation(np.resize(levels, 8))
        for g in range(8):
            far = levels[np.abs(levels - a[p, g]) >= 10]
            a[p, g + 8] = far[np.random.randint(len(far))]
    return np.exp2(a.ravel()).repeat(32)


def f64(x):
    return np.asarray(x).astype(np.float64)


def striped(idx):
    return np.tile(idx.reshape(-1, 16).T, (8, 1)).astype(np.uint16)


def unstriped(offs):
    return offs[:16].T.reshape(-1).astype(np.int64)


def pack_weight(w):
    k, n = w.shape
    w = f64(np.asarray(w, np.float32).astype(ml_dtypes.bfloat16)).reshape(k // 32, 32, n)
    amax = np.abs(w).max(1)
    byte = np.clip(np.where(amax > 0, np.frexp(amax)[1] - 1 + 127 - 7, 1), 1, 254)
    scaled = (w * np.exp2(127.0 - byte)[:, None, :]).reshape(k, n).astype(np.float32)
    words = np.ascontiguousarray(scaled.reshape(k // 512, 128, 4, n).transpose(0, 1, 3, 2)).astype(ml_dtypes.float8_e4m3fn).view(np.uint8)
    return words, np.ascontiguousarray(byte.astype(np.uint8).reshape(k // 512, 16, n))


def unpack_weight(words, scales):
    g, p, n, _ = words.shape
    vals = np.ascontiguousarray(words).view(ml_dtypes.float8_e4m3fn).astype(np.float64) * np.repeat(np.exp2(scales.astype(np.float64) - 127.0), 8, axis=1)[..., None]
    return vals.transpose(0, 1, 3, 2).reshape(g * 512, n)


def silu(v):
    return v / (1.0 + np.exp(-np.maximum(v, -700.0)))


K, T, S, N = 1024, 2048, 512, 256


def setup_inputs():
    n = np.random.standard_normal
    s = mx_kscale(K)[:, None]
    packed_xT = pack_weight(n((K, T)) * s)
    return {
        "x_words": packed_xT[0],
        "x_scales": packed_xT[1],
        "side": n((N, T)).astype(np.float32),
        "w1": (n((K, N)) / np.sqrt(K) / s).astype(np.float32),
        "offs": striped(np.random.permutation(T)[:S]),
    }


def reference(x_words, x_scales, side, w1, offs):
    xq = unpack_weight(x_words, x_scales)[:, unstriped(offs)]
    y = mxq(f64(w1), 0, "e4m3").T @ xq
    g = f64(side)[:, unstriped(offs)]
    return y * silu(g)

@@ -1,0 +1,100 @@
+from contextlib import ExitStack
+
+import concourse.mybir as mybir
+
+K, T, S, N = 1024, 2048, 512, 256
+FLOPS = 2 * K * N * S
+
+F32 = mybir.dt.float32
+BF16 = mybir.dt.bfloat16
+I32 = mybir.dt.int32
+U32 = mybir.dt.uint32
+U16 = mybir.dt.uint16
+U8 = mybir.dt.uint8
+FP8X4 = mybir.dt.float8_e4m3fn_x4
+SILU = mybir.ActivationFunctionType.Silu
+MULT = mybir.AluOpType.mult
+
+P = 128
+PACK = 4
+PASSES = K // (P * PACK)
+BLOCKS = N // P
+HALF = S // 2
+
+
+def tile_picked_sidegate_silu_p_kernel(tc, x_words, x_scales, side, w1, offs, out):
+    nc = tc.nc
+    with ExitStack() as ctx:
+        keep = ctx.enter_context(tc.tile_pool(name="keep", bufs=1))
+        psum = ctx.enter_context(tc.psum_pool(name="psum", bufs=1))
+
+        offsets = keep.tile([P, S // 16], U16, name="offsets")
+        nc.sync.dma_start(offsets[:], offs)
+
+        warm = keep.tile([P, 8], F32, name="warm")
+        warm2 = keep.tile([P, 8], F32, name="warm2")
+        nc.vector.memset(warm[:], 0.0)
+        nc.scalar.activation(warm2[:], warm[:], SILU)
+
+        scale_table = keep.tile([P, T], U8, name="scale_table", align_bytes=64)
+        nc.gpsimd.memset(scale_table[:].bitcast(I32), 0)
+        for q in range(4):
+            nc.gpsimd.dma_start(
+                out=scale_table[32 * q : 32 * q + 4 * PASSES, :].bitcast(I32),
+                in_=x_scales[:, 4 * q : 4 * q + 4, :].bitcast(I32),
+            )
+
+        w_raw = keep.tile([P, PASSES, PACK, N], F32, name="w_raw")
+        nc.sync.dma_start(out=w_raw[:], in_=w1.rearrange("(g p j) m -> p g j m", g=PASSES, j=PACK))
+        word_table = []
+        for g in range(PASSES):
+            t = keep.tile([P, T], U32, name=f"word_table{g}", align_bytes=64)
+            nc.sync.dma_start(out=t[:].bitcast(I32), in_=x_words[g].rearrange("p n t -> p (n t)").bitcast(I32))
+            word_table.append(t)
+        side_rows = []
+        for b in range(BLOCKS):
+            t = keep.tile([P, T], F32, name=f"side_rows{b}", align_bytes=64)
+            nc.sync.dma_start(out=t[:], in_=side[b * P : (b + 1) * P, :])
+            side_rows.append(t)
+
+        w_bf = keep.tile([P, PASSES, N, PACK], BF16, name="w_bf", align_bytes=64)
+        for g in range(PASSES):
+            nc.vector.tensor_copy(out=w_bf[:, g], in_=w_raw[:, g].rearrange("p j m -> p m j"))
+        w_codes = keep.tile([P, PASSES * N], U32, name="w_codes", align_bytes=64)
+        w_scales = keep.tile([P, PASSES * N], U8, name="w_scales", align_bytes=64)
+        nc.vector.quantize_mx(
+            out=w_codes[:].bitcast(FP8X4), scales=w_scales[:], in_=w_bf[:].rearrange("p g m j -> p (g m j)")
+        )
+
+        x_scale = keep.tile([P, S], U8, name="x_scale", align_bytes=64)
+        acc = [psum.tile([P, S], F32, name=f"acc{b}") for b in range(BLOCKS)]
+        for g in range(PASSES):
+            x_codes = keep.tile([P, S], U32, name=f"x_codes{g}", align_bytes=64)
+            nc.vector.tensor_copy(x_codes[:], word_table[g][:].indirect(offsets[:]))
+            if g == 0:
+                nc.vector.tensor_copy(x_scale[:], scale_table[:].indirect(offsets[:]))
+            for b in range(BLOCKS):
+                cols = slice(g * N + b * P, g * N + (b + 1) * P)
+                nc.tensor.matmul_mx(
+                    out=acc[b][:],
+                    lhsT=w_codes[:, cols].bitcast(FP8X4),
+                    lhsT_scale=w_scales[:, cols],
+                    rhs=x_codes[:].bitcast(FP8X4),
+                    rhs_scale=x_scale[4 * g : P, :],
+                    start=(g == 0),
+                    stop=(g == PASSES - 1),
+                )
+
+        for b in range(BLOCKS):
+            gates = []
+            for h in range(2):
+                picked = keep.tile([P, HALF], F32, name=f"picked{b}{h}")
+                nc.vector.tensor_copy(picked[:], side_rows[b][:].indirect(offsets[:, h * HALF // 16 : (h + 1) * HALF // 16]))
+                gate = keep.tile([P, HALF], F32, name=f"gate{b}{h}")
+                nc.scalar.activation(gate[:], picked[:], SILU)
+                gates.append(gate)
+            for h in range(2):
+                cols = slice(h * HALF, (h + 1) * HALF)
+                res = keep.tile([P, HALF], F32, name=f"res{b}{h}")
+                nc.vector.tensor_tensor(res[:], acc[b][:, cols], gates[h][:], MULT)
+                nc.sync.dma_start(out=out[b * P : (b + 1) * P, cols], in_=res[:])

@@ -31,21 +31,16 @@ def tile_picked_sidegate_silu_p_kernel(tc, x_words, x_scales, side, w1, offs, ou
         offsets = keep.tile([P, S // 16], U16, name="offsets")
         nc.sync.dma_start(offsets[:], offs)
 
-        warm = keep.tile([P, 8], F32, name="warm")
-        warm2 = keep.tile([P, 8], F32, name="warm2")
-        nc.vector.memset(warm[:], 0.0)
-        nc.scalar.activation(warm2[:], warm[:], SILU)
-
         scale_table = keep.tile([P, T], U8, name="scale_table", align_bytes=64)
         nc.gpsimd.memset(scale_table[:].bitcast(I32), 0)
+        w_raw = keep.tile([P, PASSES, PACK, N], F32, name="w_raw")
+        nc.sync.dma_start(out=w_raw[:], in_=w1.rearrange("(g p j) m -> p g j m", g=PASSES, j=PACK))
         for q in range(4):
-            nc.gpsimd.dma_start(
+            nc.sync.dma_start(
                 out=scale_table[32 * q : 32 * q + 4 * PASSES, :].bitcast(I32),
                 in_=x_scales[:, 4 * q : 4 * q + 4, :].bitcast(I32),
             )
 
-        w_raw = keep.tile([P, PASSES, PACK, N], F32, name="w_raw")
-        nc.sync.dma_start(out=w_raw[:], in_=w1.rearrange("(g p j) m -> p g j m", g=PASSES, j=PACK))
         word_table = []
         for g in range(PASSES):
             t = keep.tile([P, T], U32, name=f"word_table{g}", align_bytes=64)
@@ -88,10 +83,9 @@ def tile_picked_sidegate_silu_p_kernel(tc, x_words, x_scales, side, w1, offs, ou
         for b in range(BLOCKS):
             gates = []
             for h in range(2):
-                picked = keep.tile([P, HALF], F32, name=f"picked{b}{h}")
-                nc.vector.tensor_copy(picked[:], side_rows[b][:].indirect(offsets[:, h * HALF // 16 : (h + 1) * HALF // 16]))
-                gate = keep.tile([P, HALF], F32, name=f"gate{b}{h}")
-                nc.scalar.activation(gate[:], picked[:], SILU)
+                gate = keep.tile([P, HALF], F32, name=f"gate{h}")
+                nc.vector.tensor_copy(gate[:], side_rows[b][:].indirect(offsets[:, h * HALF // 16 : (h + 1) * HALF // 16]))
+                nc.scalar.activation(gate[:], gate[:], SILU)
                 gates.append(gate)
             for h in range(2):
                 cols = slice(h * HALF, (h + 1) * HALF)

@@ -12,7 +12,7 @@ U32 = mybir.dt.uint32
 U16 = mybir.dt.uint16
 U8 = mybir.dt.uint8
 FP8X4 = mybir.dt.float8_e4m3fn_x4
-SILU = mybir.ActivationFunctionType.Silu
+SIGMOID = mybir.ActivationFunctionType.Sigmoid
 MULT = mybir.AluOpType.mult
 
 P = 128
@@ -29,12 +29,12 @@ def tile_picked_sidegate_silu_p_kernel(tc, x_words, x_scales, side, w1, offs, ou
         psum = ctx.enter_context(tc.psum_pool(name="psum", bufs=1))
 
         offsets = keep.tile([P, S // 16], U16, name="offsets")
-        nc.sync.dma_start(offsets[:], offs)
 
         scale_table = keep.tile([P, T], U8, name="scale_table", align_bytes=64)
         nc.gpsimd.memset(scale_table[:].bitcast(I32), 0)
         w_raw = keep.tile([P, PASSES, PACK, N], F32, name="w_raw")
         nc.sync.dma_start(out=w_raw[:], in_=w1.rearrange("(g p j) m -> p g j m", g=PASSES, j=PACK))
+        nc.sync.dma_start(offsets[:], offs)
         for q in range(4):
             nc.sync.dma_start(
                 out=scale_table[32 * q : 32 * q + 4 * PASSES, :].bitcast(I32),
@@ -54,41 +54,48 @@ def tile_picked_sidegate_silu_p_kernel(tc, x_words, x_scales, side, w1, offs, ou
 
         w_bf = keep.tile([P, PASSES, N, PACK], BF16, name="w_bf", align_bytes=64)
         for g in range(PASSES):
-            nc.vector.tensor_copy(out=w_bf[:, g], in_=w_raw[:, g].rearrange("p j m -> p m j"))
+            nc.scalar.copy(out=w_bf[:, g], in_=w_raw[:, g].rearrange("p j m -> p m j"))
         w_codes = keep.tile([P, PASSES * N], U32, name="w_codes", align_bytes=64)
         w_scales = keep.tile([P, PASSES * N], U8, name="w_scales", align_bytes=64)
         nc.vector.quantize_mx(
             out=w_codes[:].bitcast(FP8X4), scales=w_scales[:], in_=w_bf[:].rearrange("p g m j -> p (g m j)")
         )
 
+        halves = [offsets[:, h * HALF // 16 : (h + 1) * HALF // 16] for h in range(2)]
         x_scale = keep.tile([P, S], U8, name="x_scale", align_bytes=64)
-        acc = [psum.tile([P, S], F32, name=f"acc{b}") for b in range(BLOCKS)]
+        nc.vector.tensor_copy(x_scale[:], scale_table[:].indirect(offsets[:]))
+        acc = [[psum.tile([P, HALF], F32, name=f"acc{b}{h}") for h in range(2)] for b in range(BLOCKS)]
+        y = [[keep.tile([P, HALF], F32, name=f"y{b}{h}") for h in range(2)] for b in range(BLOCKS)]
         for g in range(PASSES):
-            x_codes = keep.tile([P, S], U32, name=f"x_codes{g}", align_bytes=64)
-            nc.vector.tensor_copy(x_codes[:], word_table[g][:].indirect(offsets[:]))
-            if g == 0:
-                nc.vector.tensor_copy(x_scale[:], scale_table[:].indirect(offsets[:]))
+            for h in range(2):
+                x_codes = keep.tile([P, HALF], U32, name=f"x_codes{g}{h}", align_bytes=64)
+                nc.vector.tensor_copy(x_codes[:], word_table[g][:].indirect(halves[h]))
+                for b in range(BLOCKS):
+                    cols = slice(g * N + b * P, g * N + (b + 1) * P)
+                    nc.tensor.matmul_mx(
+                        out=acc[b][h][:],
+                        lhsT=w_codes[:, cols].bitcast(FP8X4),
+                        lhsT_scale=w_scales[:, cols],
+                        rhs=x_codes[:].bitcast(FP8X4),
+                        rhs_scale=x_scale[4 * g : P, h * HALF : (h + 1) * HALF],
+                        start=(g == 0),
+                        stop=(g == PASSES - 1),
+                    )
+        for h in range(2):
             for b in range(BLOCKS):
-                cols = slice(g * N + b * P, g * N + (b + 1) * P)
-                nc.tensor.matmul_mx(
-                    out=acc[b][:],
-                    lhsT=w_codes[:, cols].bitcast(FP8X4),
-                    lhsT_scale=w_scales[:, cols],
-                    rhs=x_codes[:].bitcast(FP8X4),
-                    rhs_scale=x_scale[4 * g : P, :],
-                    start=(g == 0),
-                    stop=(g == PASSES - 1),
-                )
+                nc.vector.tensor_copy(y[b][h][:], acc[b][h][:])
 
         for b in range(BLOCKS):
-            gates = []
+            parts = []
             for h in range(2):
-                gate = keep.tile([P, HALF], F32, name=f"gate{h}")
-                nc.vector.tensor_copy(gate[:], side_rows[b][:].indirect(offsets[:, h * HALF // 16 : (h + 1) * HALF // 16]))
-                nc.scalar.activation(gate[:], gate[:], SILU)
-                gates.append(gate)
+                picked = side_rows[b][:].indirect(halves[h])
+                sig = keep.tile([P, HALF], F32, name=f"sig{b}{h}")
+                nc.scalar.activation(sig[:], picked, SIGMOID)
+                prod = keep.tile([P, HALF], F32, name=f"prod{h}")
+                nc.vector.tensor_tensor(prod[:], picked, y[b][h][:], MULT)
+                parts.append((sig, prod))
             for h in range(2):
                 cols = slice(h * HALF, (h + 1) * HALF)
                 res = keep.tile([P, HALF], F32, name=f"res{b}{h}")
-                nc.vector.tensor_tensor(res[:], acc[b][:, cols], gates[h][:], MULT)
+                nc.vector.tensor_tensor(res[:], parts[h][1][:], parts[h][0][:], MULT)
                 nc.sync.dma_start(out=out[b * P : (b + 1) * P, cols], in_=res[:])

@@ -32,20 +32,26 @@ def tile_picked_sidegate_silu_p_kernel(tc, x_words, x_scales, side, w1, offs, ou
 
         scale_table = keep.tile([P, T], U8, name="scale_table", align_bytes=64)
         nc.gpsimd.memset(scale_table[:].bitcast(I32), 0)
+        def load_scale_row(r):
+            for g in range(PASSES):
+                nc.sync.dma_start(
+                    out=scale_table[4 * g + r : P : 32, :].bitcast(I32), in_=x_scales[g, r : 16 : 4, :].bitcast(I32)
+                )
+
+        word_table = [keep.tile([P, T], U32, name=f"word_table{g}", align_bytes=64) for g in range(PASSES)]
+
+        def load_words(g):
+            nc.sync.dma_start(out=word_table[g][:].bitcast(I32), in_=x_words[g].rearrange("p n t -> p (n t)").bitcast(I32))
+
         w_raw = keep.tile([P, PASSES, PACK, N], F32, name="w_raw")
         nc.sync.dma_start(out=w_raw[:], in_=w1.rearrange("(g p j) m -> p g j m", g=PASSES, j=PACK))
+        for r in range(2):
+            load_scale_row(r)
         nc.sync.dma_start(offsets[:], offs)
-        for q in range(4):
-            nc.sync.dma_start(
-                out=scale_table[32 * q : 32 * q + 4 * PASSES, :].bitcast(I32),
-                in_=x_scales[:, 4 * q : 4 * q + 4, :].bitcast(I32),
-            )
-
-        word_table = []
-        for g in range(PASSES):
-            t = keep.tile([P, T], U32, name=f"word_table{g}", align_bytes=64)
-            nc.sync.dma_start(out=t[:].bitcast(I32), in_=x_words[g].rearrange("p n t -> p (n t)").bitcast(I32))
-            word_table.append(t)
+        load_words(0)
+        for r in range(2, 4):
+            load_scale_row(r)
+        load_words(1)
         side_rows = []
         for b in range(BLOCKS):
             t = keep.tile([P, T], F32, name=f"side_rows{b}", align_bytes=64)
@@ -53,8 +59,8 @@ def tile_picked_sidegate_silu_p_kernel(tc, x_words, x_scales, side, w1, offs, ou
             side_rows.append(t)
 
         w_bf = keep.tile([P, PASSES, N, PACK], BF16, name="w_bf", align_bytes=64)
-        for g in range(PASSES):
-            nc.scalar.copy(out=w_bf[:, g], in_=w_raw[:, g].rearrange("p j m -> p m j"))
+        nc.scalar.copy(out=w_bf[:, 0], in_=w_raw[:, 0].rearrange("p j m -> p m j"))
+        nc.vector.tensor_copy(out=w_bf[:, 1], in_=w_raw[:, 1].rearrange("p j m -> p m j"))
         w_codes = keep.tile([P, PASSES * N], U32, name="w_codes", align_bytes=64)
         w_scales = keep.tile([P, PASSES * N], U8, name="w_scales", align_bytes=64)
         nc.vector.quantize_mx(
@@ -62,27 +68,28 @@ def tile_picked_sidegate_silu_p_kernel(tc, x_words, x_scales, side, w1, offs, ou
         )
 
         halves = [offsets[:, h * HALF // 16 : (h + 1) * HALF // 16] for h in range(2)]
-        x_scale = keep.tile([P, S], U8, name="x_scale", align_bytes=64)
-        nc.vector.tensor_copy(x_scale[:], scale_table[:].indirect(offsets[:]))
+        x_scale = [keep.tile([P, HALF], U8, name=f"x_scale{h}", align_bytes=64) for h in range(2)]
         acc = [[psum.tile([P, HALF], F32, name=f"acc{b}{h}") for h in range(2)] for b in range(BLOCKS)]
         y = [[keep.tile([P, HALF], F32, name=f"y{b}{h}") for h in range(2)] for b in range(BLOCKS)]
+        x_codes = [[keep.tile([P, HALF], U32, name=f"x_codes{g}{h}", align_bytes=64) for h in range(2)] for g in range(PASSES)]
         for g in range(PASSES):
             for h in range(2):
-                x_codes = keep.tile([P, HALF], U32, name=f"x_codes{g}{h}", align_bytes=64)
-                nc.vector.tensor_copy(x_codes[:], word_table[g][:].indirect(halves[h]))
+                nc.vector.tensor_copy(x_codes[g][h][:], word_table[g][:].indirect(halves[h]))
+                if g == 0:
+                    nc.vector.tensor_copy(x_scale[h][:], scale_table[:].indirect(halves[h]))
                 for b in range(BLOCKS):
                     cols = slice(g * N + b * P, g * N + (b + 1) * P)
                     nc.tensor.matmul_mx(
                         out=acc[b][h][:],
                         lhsT=w_codes[:, cols].bitcast(FP8X4),
                         lhsT_scale=w_scales[:, cols],
-                        rhs=x_codes[:].bitcast(FP8X4),
-                        rhs_scale=x_scale[4 * g : P, h * HALF : (h + 1) * HALF],
+                        rhs=x_codes[g][h][:].bitcast(FP8X4),
+                        rhs_scale=x_scale[h][4 * g : P, :],
                         start=(g == 0),
                         stop=(g == PASSES - 1),
                     )
-        for h in range(2):
-            for b in range(BLOCKS):
+        for b in range(BLOCKS):
+            for h in range(2):
                 nc.vector.tensor_copy(y[b][h][:], acc[b][h][:])
 
         for b in range(BLOCKS):

@@ -29,78 +29,104 @@ def tile_picked_sidegate_silu_p_kernel(tc, x_words, x_scales, side, w1, offs, ou
         psum = ctx.enter_context(tc.psum_pool(name="psum", bufs=1))
 
         offsets = keep.tile([P, S // 16], U16, name="offsets")
+        scale_table = keep.tile([P, T], U8, name="scale_table", tag="first", align_bytes=64)
+        nc.vector.memset(scale_table[32:64, :].bitcast(I32), 0)
+        nc.vector.memset(scale_table[64:P, :].bitcast(I32), 0)
+        x_scale = [keep.tile([P, S], U8, name=f"x_scale{g}", align_bytes=64) for g in range(PASSES)]
+        for g in range(PASSES):
+            nc.gpsimd.memset(x_scale[g][:].bitcast(I32), 0)
+        word_table = []
+        side_rows = []
+        w_raw = keep.tile([P, PASSES, PACK, N], F32, name="w_raw", tag="side0", align_bytes=64)
 
-        scale_table = keep.tile([P, T], U8, name="scale_table", align_bytes=64)
-        nc.gpsimd.memset(scale_table[:].bitcast(I32), 0)
-        def load_scale_row(r):
-            for g in range(PASSES):
+        def load_words(g, cols):
+            words = x_words[g].rearrange("p n t -> p (n t)").bitcast(I32)
+            nc.sync.dma_start(out=word_table[g][:].bitcast(I32)[:, cols], in_=words[:, cols])
+
+        def load_side(b):
+            nc.sync.dma_start(out=side_rows[b][:], in_=side[b * P : (b + 1) * P, :])
+
+        def load_w():
+            nc.sync.dma_start(out=w_raw[:], in_=w1.rearrange("(g p j) m -> p g j m", g=PASSES, j=PACK))
+
+        nc.sync.dma_start(out=scale_table[0:32, :].bitcast(I32), in_=x_scales.rearrange("g q c -> (g q) c").bitcast(I32))
+        nc.sync.dma_start(offsets[:], offs)
+        load_w()
+        word_table.append(keep.tile([P, T], U32, name="word_table0", tag="words0", align_bytes=64))
+        load_words(0, slice(0, T))
+
+        picked_scale = keep.tile([P, S], U8, name="picked_scale", align_bytes=64)
+        nc.vector.tensor_copy(picked_scale[:], scale_table[:].indirect(offsets[:]))
+
+        def move_scales(g):
+            for r in range(4):
                 nc.sync.dma_start(
-                    out=scale_table[4 * g + r : P : 32, :].bitcast(I32), in_=x_scales[g, r : 16 : 4, :].bitcast(I32)
+                    out=x_scale[g][4 * g + r : P : 32, :].bitcast(I32),
+                    in_=picked_scale[16 * g + r : 16 * (g + 1) : 4, :].bitcast(I32),
                 )
 
-        word_table = [keep.tile([P, T], U32, name=f"word_table{g}", align_bytes=64) for g in range(PASSES)]
-
-        def load_words(g):
-            nc.sync.dma_start(out=word_table[g][:].bitcast(I32), in_=x_words[g].rearrange("p n t -> p (n t)").bitcast(I32))
-
-        w_raw = keep.tile([P, PASSES, PACK, N], F32, name="w_raw")
-        nc.sync.dma_start(out=w_raw[:], in_=w1.rearrange("(g p j) m -> p g j m", g=PASSES, j=PACK))
-        for r in range(2):
-            load_scale_row(r)
-        nc.sync.dma_start(offsets[:], offs)
-        load_words(0)
-        for r in range(2, 4):
-            load_scale_row(r)
-        load_words(1)
-        side_rows = []
-        for b in range(BLOCKS):
-            t = keep.tile([P, T], F32, name=f"side_rows{b}", align_bytes=64)
-            nc.sync.dma_start(out=t[:], in_=side[b * P : (b + 1) * P, :])
-            side_rows.append(t)
-
-        w_bf = keep.tile([P, PASSES, N, PACK], BF16, name="w_bf", align_bytes=64)
-        nc.scalar.copy(out=w_bf[:, 0], in_=w_raw[:, 0].rearrange("p j m -> p m j"))
-        nc.vector.tensor_copy(out=w_bf[:, 1], in_=w_raw[:, 1].rearrange("p j m -> p m j"))
-        w_codes = keep.tile([P, PASSES * N], U32, name="w_codes", align_bytes=64)
-        w_scales = keep.tile([P, PASSES * N], U8, name="w_scales", align_bytes=64)
-        nc.vector.quantize_mx(
-            out=w_codes[:].bitcast(FP8X4), scales=w_scales[:], in_=w_bf[:].rearrange("p g m j -> p (g m j)")
-        )
+        move_scales(0)
+        word_table.append(keep.tile([P, T], U32, name="word_table1", tag="first", align_bytes=64))
+        load_words(1, slice(0, T))
+        move_scales(1)
 
         halves = [offsets[:, h * HALF // 16 : (h + 1) * HALF // 16] for h in range(2)]
-        x_scale = [keep.tile([P, HALF], U8, name=f"x_scale{h}", align_bytes=64) for h in range(2)]
+
+        warm = keep.tile([P, 1], F32, name="warm")
+        nc.scalar.activation(warm[:], w_raw[:, 0, 0, 0:1], SIGMOID)
+
+        w_bf = [keep.tile([P, N, PACK], BF16, name=f"w_bf{g}", tag=f"bf{g}", align_bytes=64) for g in range(PASSES)]
+        nc.scalar.copy(out=w_bf[0][:], in_=w_raw[:, 0].rearrange("p j m -> p m j"))
+        nc.vector.tensor_copy(out=w_bf[1][:], in_=w_raw[:, 1].rearrange("p j m -> p m j"))
+        side_rows.append(keep.tile([P, T], F32, name="side_rows0", tag="side0", align_bytes=64))
+        load_side(0)
+        w_codes = keep.tile([P, PASSES * N], U32, name="w_codes", align_bytes=64)
+        w_scales = keep.tile([P, PASSES * N], U8, name="w_scales", align_bytes=64)
+        for g in reversed(range(PASSES)):
+            cols = slice(g * N, (g + 1) * N)
+            nc.vector.quantize_mx(
+                out=w_codes[:, cols].bitcast(FP8X4), scales=w_scales[:, cols], in_=w_bf[g][:].rearrange("p m j -> p (m j)")
+            )
+        side_rows.append(keep.tile([P, T], F32, name="side_rows1", tag="bf1", align_bytes=64))
+        load_side(1)
+
         acc = [[psum.tile([P, HALF], F32, name=f"acc{b}{h}") for h in range(2)] for b in range(BLOCKS)]
-        y = [[keep.tile([P, HALF], F32, name=f"y{b}{h}") for h in range(2)] for b in range(BLOCKS)]
-        x_codes = [[keep.tile([P, HALF], U32, name=f"x_codes{g}{h}", align_bytes=64) for h in range(2)] for g in range(PASSES)]
+
         for g in range(PASSES):
+            x_codes = keep.tile([P, S], U32, name=f"x_codes{g}", tag=("bf0", "words0")[g], align_bytes=64)
             for h in range(2):
-                nc.vector.tensor_copy(x_codes[g][h][:], word_table[g][:].indirect(halves[h]))
-                if g == 0:
-                    nc.vector.tensor_copy(x_scale[h][:], scale_table[:].indirect(halves[h]))
+                entries = slice(h * HALF, (h + 1) * HALF)
+                nc.vector.tensor_copy(x_codes[:, entries], word_table[g][:].indirect(halves[h]))
                 for b in range(BLOCKS):
                     cols = slice(g * N + b * P, g * N + (b + 1) * P)
                     nc.tensor.matmul_mx(
                         out=acc[b][h][:],
                         lhsT=w_codes[:, cols].bitcast(FP8X4),
                         lhsT_scale=w_scales[:, cols],
-                        rhs=x_codes[g][h][:].bitcast(FP8X4),
-                        rhs_scale=x_scale[h][4 * g : P, :],
+                        rhs=x_codes[:, entries].bitcast(FP8X4),
+                        rhs_scale=x_scale[g][4 * g : P, entries],
                         start=(g == 0),
                         stop=(g == PASSES - 1),
                     )
-        for b in range(BLOCKS):
-            for h in range(2):
-                nc.vector.tensor_copy(y[b][h][:], acc[b][h][:])
+
+        y = [[keep.tile([P, HALF], F32, name=f"y0{h}")[:] for h in range(2)]]
+        for h in range(2):
+            nc.vector.tensor_copy(y[0][h], acc[0][h][:])
 
         for b in range(BLOCKS):
             parts = []
             for h in range(2):
                 picked = side_rows[b][:].indirect(halves[h])
-                sig = keep.tile([P, HALF], F32, name=f"sig{b}{h}")
+                sig = keep.tile([P, HALF], F32, name=f"sig{h}")
                 nc.scalar.activation(sig[:], picked, SIGMOID)
                 prod = keep.tile([P, HALF], F32, name=f"prod{h}")
-                nc.vector.tensor_tensor(prod[:], picked, y[b][h][:], MULT)
+                nc.vector.tensor_tensor(prod[:], picked, y[b][h], MULT)
                 parts.append((sig, prod))
+            if b == 0:
+                y1 = keep.tile([P, S], F32, name="y1", tag="side0", align_bytes=64)
+                y.append([y1[:, h * HALF : (h + 1) * HALF] for h in range(2)])
+                for h in range(2):
+                    nc.scalar.copy(out=y[1][h], in_=acc[1][h][:])
             for h in range(2):
                 cols = slice(h * HALF, (h + 1) * HALF)
                 res = keep.tile([P, HALF], F32, name=f"res{b}{h}")

@@ -32,9 +32,8 @@ def tile_picked_sidegate_silu_p_kernel(tc, x_words, x_scales, side, w1, offs, ou
         scale_table = keep.tile([P, T], U8, name="scale_table", tag="first", align_bytes=64)
         nc.vector.memset(scale_table[32:64, :].bitcast(I32), 0)
         nc.vector.memset(scale_table[64:P, :].bitcast(I32), 0)
-        x_scale = [keep.tile([P, S], U8, name=f"x_scale{g}", align_bytes=64) for g in range(PASSES)]
-        for g in range(PASSES):
-            nc.gpsimd.memset(x_scale[g][:].bitcast(I32), 0)
+        x_scale = keep.tile([P, S], U8, name="x_scale", align_bytes=64)
+        nc.gpsimd.memset(x_scale[:].bitcast(I32), 0)
         word_table = []
         side_rows = []
         w_raw = keep.tile([P, PASSES, PACK, N], F32, name="w_raw", tag="side0", align_bytes=64)
@@ -49,7 +48,11 @@ def tile_picked_sidegate_silu_p_kernel(tc, x_words, x_scales, side, w1, offs, ou
         def load_w():
             nc.sync.dma_start(out=w_raw[:], in_=w1.rearrange("(g p j) m -> p g j m", g=PASSES, j=PACK))
 
-        nc.sync.dma_start(out=scale_table[0:32, :].bitcast(I32), in_=x_scales.rearrange("g q c -> (g q) c").bitcast(I32))
+        for g in range(PASSES):
+            nc.sync.dma_start(
+                out=scale_table[16 * g : 16 * (g + 1), :].bitcast(I32),
+                in_=x_scales[g].rearrange("(q r) c -> r q c", r=4).bitcast(I32),
+            )
         nc.sync.dma_start(offsets[:], offs)
         load_w()
         word_table.append(keep.tile([P, T], U32, name="word_table0", tag="words0", align_bytes=64))
@@ -58,22 +61,12 @@ def tile_picked_sidegate_silu_p_kernel(tc, x_words, x_scales, side, w1, offs, ou
         picked_scale = keep.tile([P, S], U8, name="picked_scale", align_bytes=64)
         nc.vector.tensor_copy(picked_scale[:], scale_table[:].indirect(offsets[:]))
 
-        def move_scales(g):
-            for r in range(4):
-                nc.sync.dma_start(
-                    out=x_scale[g][4 * g + r : P : 32, :].bitcast(I32),
-                    in_=picked_scale[16 * g + r : 16 * (g + 1) : 4, :].bitcast(I32),
-                )
-
-        move_scales(0)
+        for q in range(4):
+            nc.sync.dma_start(out=x_scale[32 * q : 32 * q + 8, :].bitcast(I32), in_=picked_scale[q:32:4, :].bitcast(I32))
         word_table.append(keep.tile([P, T], U32, name="word_table1", tag="first", align_bytes=64))
         load_words(1, slice(0, T))
-        move_scales(1)
 
         halves = [offsets[:, h * HALF // 16 : (h + 1) * HALF // 16] for h in range(2)]
-
-        warm = keep.tile([P, 1], F32, name="warm")
-        nc.scalar.activation(warm[:], w_raw[:, 0, 0, 0:1], SIGMOID)
 
         w_bf = [keep.tile([P, N, PACK], BF16, name=f"w_bf{g}", tag=f"bf{g}", align_bytes=64) for g in range(PASSES)]
         nc.scalar.copy(out=w_bf[0][:], in_=w_raw[:, 0].rearrange("p j m -> p m j"))
@@ -104,7 +97,7 @@ def tile_picked_sidegate_silu_p_kernel(tc, x_words, x_scales, side, w1, offs, ou
                         lhsT=w_codes[:, cols].bitcast(FP8X4),
                         lhsT_scale=w_scales[:, cols],
                         rhs=x_codes[:, entries].bitcast(FP8X4),
-                        rhs_scale=x_scale[g][4 * g : P, entries],
+                        rhs_scale=x_scale[4 * g : P, entries],
                         start=(g == 0),
                         stop=(g == PASSES - 1),
                     )

@@ -19,6 +19,10 @@ P = 128
 PACK = 4
 PASSES = K // (P * PACK)
 BLOCKS = N // P
+QUADRANT = 32
+QUADRANTS = P // QUADRANT
+ROWS = 4
+GROUP = 16
 HALF = S // 2
 
 
@@ -28,51 +32,50 @@ def tile_picked_sidegate_silu_p_kernel(tc, x_words, x_scales, side, w1, offs, ou
         keep = ctx.enter_context(tc.tile_pool(name="keep", bufs=1))
         psum = ctx.enter_context(tc.psum_pool(name="psum", bufs=1))
 
-        offsets = keep.tile([P, S // 16], U16, name="offsets")
+        offsets = keep.tile([P, S // GROUP], U16, name="offsets")
+
         scale_table = keep.tile([P, T], U8, name="scale_table", tag="first", align_bytes=64)
-        nc.vector.memset(scale_table[32:64, :].bitcast(I32), 0)
-        nc.vector.memset(scale_table[64:P, :].bitcast(I32), 0)
+        nc.vector.memset(scale_table[QUADRANT : 2 * QUADRANT, :].bitcast(I32), 0)
+        nc.vector.memset(scale_table[2 * QUADRANT : P, :].bitcast(I32), 0)
         x_scale = keep.tile([P, S], U8, name="x_scale", align_bytes=64)
         nc.gpsimd.memset(x_scale[:].bitcast(I32), 0)
-        word_table = []
-        side_rows = []
         w_raw = keep.tile([P, PASSES, PACK, N], F32, name="w_raw", tag="side0", align_bytes=64)
 
-        def load_words(g, cols):
-            words = x_words[g].rearrange("p n t -> p (n t)").bitcast(I32)
-            nc.sync.dma_start(out=word_table[g][:].bitcast(I32)[:, cols], in_=words[:, cols])
+        def load_words(g, tag):
+            table = keep.tile([P, T], U32, name=f"word_table{g}", tag=tag, align_bytes=64)
+            nc.sync.dma_start(out=table[:].bitcast(I32), in_=x_words[g].rearrange("p n t -> p (n t)").bitcast(I32))
+            return table
 
-        def load_side(b):
-            nc.sync.dma_start(out=side_rows[b][:], in_=side[b * P : (b + 1) * P, :])
+        def load_side(b, tag):
+            rows = keep.tile([P, T], F32, name=f"side_rows{b}", tag=tag, align_bytes=64)
+            nc.sync.dma_start(out=rows[:], in_=side[b * P : (b + 1) * P, :])
+            return rows
 
-        def load_w():
-            nc.sync.dma_start(out=w_raw[:], in_=w1.rearrange("(g p j) m -> p g j m", g=PASSES, j=PACK))
-
-        for g in range(PASSES):
+        pass_rows = ROWS * QUADRANTS
+        for g in reversed(range(PASSES)):
             nc.sync.dma_start(
-                out=scale_table[16 * g : 16 * (g + 1), :].bitcast(I32),
-                in_=x_scales[g].rearrange("(q r) c -> r q c", r=4).bitcast(I32),
+                out=scale_table[pass_rows * g : pass_rows * (g + 1), :].bitcast(I32),
+                in_=x_scales[g].rearrange("(q r) c -> r q c", r=ROWS).bitcast(I32),
             )
         nc.sync.dma_start(offsets[:], offs)
-        load_w()
-        word_table.append(keep.tile([P, T], U32, name="word_table0", tag="words0", align_bytes=64))
-        load_words(0, slice(0, T))
+        nc.sync.dma_start(out=w_raw[:], in_=w1.rearrange("(g p j) m -> p g j m", g=PASSES, j=PACK))
+        word_table = [load_words(0, "words0")]
 
         picked_scale = keep.tile([P, S], U8, name="picked_scale", align_bytes=64)
         nc.vector.tensor_copy(picked_scale[:], scale_table[:].indirect(offsets[:]))
+        for q in range(QUADRANTS):
+            nc.sync.dma_start(
+                out=x_scale[QUADRANT * q : QUADRANT * q + ROWS * PASSES, :].bitcast(I32),
+                in_=picked_scale[q:QUADRANT:QUADRANTS, :].bitcast(I32),
+            )
+        word_table.append(load_words(1, "first"))
 
-        for q in range(4):
-            nc.sync.dma_start(out=x_scale[32 * q : 32 * q + 8, :].bitcast(I32), in_=picked_scale[q:32:4, :].bitcast(I32))
-        word_table.append(keep.tile([P, T], U32, name="word_table1", tag="first", align_bytes=64))
-        load_words(1, slice(0, T))
-
-        halves = [offsets[:, h * HALF // 16 : (h + 1) * HALF // 16] for h in range(2)]
+        halves = [offsets[:, h * HALF // GROUP : (h + 1) * HALF // GROUP] for h in range(2)]
 
         w_bf = [keep.tile([P, N, PACK], BF16, name=f"w_bf{g}", tag=f"bf{g}", align_bytes=64) for g in range(PASSES)]
         nc.scalar.copy(out=w_bf[0][:], in_=w_raw[:, 0].rearrange("p j m -> p m j"))
         nc.vector.tensor_copy(out=w_bf[1][:], in_=w_raw[:, 1].rearrange("p j m -> p m j"))
-        side_rows.append(keep.tile([P, T], F32, name="side_rows0", tag="side0", align_bytes=64))
-        load_side(0)
+        side_rows = [load_side(0, "side0")]
         w_codes = keep.tile([P, PASSES * N], U32, name="w_codes", align_bytes=64)
         w_scales = keep.tile([P, PASSES * N], U8, name="w_scales", align_bytes=64)
         for g in reversed(range(PASSES)):
@@ -80,8 +83,7 @@ def tile_picked_sidegate_silu_p_kernel(tc, x_words, x_scales, side, w1, offs, ou
             nc.vector.quantize_mx(
                 out=w_codes[:, cols].bitcast(FP8X4), scales=w_scales[:, cols], in_=w_bf[g][:].rearrange("p m j -> p (m j)")
             )
-        side_rows.append(keep.tile([P, T], F32, name="side_rows1", tag="bf1", align_bytes=64))
-        load_side(1)
+        side_rows.append(load_side(1, "bf1"))
 
         acc = [[psum.tile([P, HALF], F32, name=f"acc{b}{h}") for h in range(2)] for b in range(BLOCKS)]
 
@@ -97,31 +99,35 @@ def tile_picked_sidegate_silu_p_kernel(tc, x_words, x_scales, side, w1, offs, ou
                         lhsT=w_codes[:, cols].bitcast(FP8X4),
                         lhsT_scale=w_scales[:, cols],
                         rhs=x_codes[:, entries].bitcast(FP8X4),
-                        rhs_scale=x_scale[4 * g : P, entries],
+                        rhs_scale=x_scale[ROWS * g : P, entries],
                         start=(g == 0),
                         stop=(g == PASSES - 1),
                     )
 
-        y = [[keep.tile([P, HALF], F32, name=f"y0{h}")[:] for h in range(2)]]
-        for h in range(2):
-            nc.vector.tensor_copy(y[0][h], acc[0][h][:])
-
-        for b in range(BLOCKS):
+        def gate(b, y):
             parts = []
             for h in range(2):
                 picked = side_rows[b][:].indirect(halves[h])
                 sig = keep.tile([P, HALF], F32, name=f"sig{h}")
                 nc.scalar.activation(sig[:], picked, SIGMOID)
                 prod = keep.tile([P, HALF], F32, name=f"prod{h}")
-                nc.vector.tensor_tensor(prod[:], picked, y[b][h], MULT)
+                nc.vector.tensor_tensor(prod[:], picked, y[h], MULT)
                 parts.append((sig, prod))
-            if b == 0:
-                y1 = keep.tile([P, S], F32, name="y1", tag="side0", align_bytes=64)
-                y.append([y1[:, h * HALF : (h + 1) * HALF] for h in range(2)])
-                for h in range(2):
-                    nc.scalar.copy(out=y[1][h], in_=acc[1][h][:])
-            for h in range(2):
-                cols = slice(h * HALF, (h + 1) * HALF)
+            return parts
+
+        def finish(b, parts):
+            for h, (sig, prod) in enumerate(parts):
                 res = keep.tile([P, HALF], F32, name=f"res{b}{h}")
-                nc.vector.tensor_tensor(res[:], parts[h][1][:], parts[h][0][:], MULT)
-                nc.sync.dma_start(out=out[b * P : (b + 1) * P, cols], in_=res[:])
+                nc.vector.tensor_tensor(res[:], prod[:], sig[:], MULT)
+                nc.sync.dma_start(out=out[b * P : (b + 1) * P, h * HALF : (h + 1) * HALF], in_=res[:])
+
+        y0 = [keep.tile([P, HALF], F32, name=f"y0{h}")[:] for h in range(2)]
+        for h in range(2):
+            nc.vector.tensor_copy(y0[h], acc[0][h][:])
+        parts0 = gate(0, y0)
+        y1_whole = keep.tile([P, S], F32, name="y1", tag="side0", align_bytes=64)
+        y1 = [y1_whole[:, h * HALF : (h + 1) * HALF] for h in range(2)]
+        for h in range(2):
+            nc.scalar.copy(out=y1[h], in_=acc[1][h][:])
+        finish(0, parts0)
+        finish(1, gate(1, y1))

@@ -32,74 +32,82 @@ def tile_picked_sidegate_silu_p_kernel(tc, x_words, x_scales, side, w1, offs, ou
         keep = ctx.enter_context(tc.tile_pool(name="keep", bufs=1))
         psum = ctx.enter_context(tc.psum_pool(name="psum", bufs=1))
 
+        over = ctx.enter_context(tc.tile_pool(name="over", bufs=1))
+
         offsets = keep.tile([P, S // GROUP], U16, name="offsets")
 
-        scale_table = keep.tile([P, T], U8, name="scale_table", tag="first", align_bytes=64)
-        nc.vector.memset(scale_table[QUADRANT : 2 * QUADRANT, :].bitcast(I32), 0)
-        nc.vector.memset(scale_table[2 * QUADRANT : P, :].bitcast(I32), 0)
-        x_scale = keep.tile([P, S], U8, name="x_scale", align_bytes=64)
+        side_bytes = 4 * T
+        scale_table = over.tile([P, PASSES, T], U8, name="scale_table", offset=side_bytes - T, align_bytes=64)
+        nc.vector.memset(scale_table[:, 0, :].bitcast(I32), 0)
+        nc.gpsimd.memset(scale_table[:, 1, :].bitcast(I32), 0)
+        x_scale = keep.tile([P, PASSES * S], U8, name="x_scale", align_bytes=64)
         nc.gpsimd.memset(x_scale[:].bitcast(I32), 0)
-        w_raw = keep.tile([P, PASSES, PACK, N], F32, name="w_raw", tag="side0", align_bytes=64)
 
-        def load_words(g, tag):
-            table = keep.tile([P, T], U32, name=f"word_table{g}", tag=tag, align_bytes=64)
+        def load_w(g):
+            raw = keep.tile([P, PACK, N], F32, name=f"w_raw{g}", align_bytes=64)
+            nc.sync.dma_start(out=raw[:], in_=w1[g * P * PACK : (g + 1) * P * PACK, :].rearrange("(p j) m -> p j m", j=PACK))
+            return raw
+
+        def load_words(g):
+            table = keep.tile([P, T], U32, name=f"word_table{g}", tag=f"words{g}", align_bytes=64)
             nc.sync.dma_start(out=table[:].bitcast(I32), in_=x_words[g].rearrange("p n t -> p (n t)").bitcast(I32))
             return table
 
-        def load_side(b, tag):
-            rows = keep.tile([P, T], F32, name=f"side_rows{b}", tag=tag, align_bytes=64)
+        def load_side(b):
+            rows = over.tile([P, T], F32, name=f"side_rows{b}", offset=b * side_bytes, align_bytes=64)
             nc.sync.dma_start(out=rows[:], in_=side[b * P : (b + 1) * P, :])
             return rows
 
-        pass_rows = ROWS * QUADRANTS
-        for g in reversed(range(PASSES)):
-            nc.sync.dma_start(
-                out=scale_table[pass_rows * g : pass_rows * (g + 1), :].bitcast(I32),
-                in_=x_scales[g].rearrange("(q r) c -> r q c", r=ROWS).bitcast(I32),
-            )
+        w_raw = [load_w(0)]
+        step = QUADRANT // ROWS
+        nc.sync.dma_start(
+            out=scale_table[0:P:step].bitcast(I32), in_=x_scales.rearrange("g i c -> i g c").bitcast(I32)
+        )
         nc.sync.dma_start(offsets[:], offs)
-        nc.sync.dma_start(out=w_raw[:], in_=w1.rearrange("(g p j) m -> p g j m", g=PASSES, j=PACK))
-        word_table = [load_words(0, "words0")]
+        w_raw.append(load_w(1))
+        word_table = [load_words(g) for g in range(PASSES)]
 
-        picked_scale = keep.tile([P, S], U8, name="picked_scale", align_bytes=64)
-        nc.vector.tensor_copy(picked_scale[:], scale_table[:].indirect(offsets[:]))
+        picked_scale = keep.tile([P, PASSES * S], U8, name="picked_scale", align_bytes=64)
+        for g in range(PASSES):
+            nc.vector.tensor_copy(picked_scale[:, g * S : (g + 1) * S], scale_table[:, g, :].indirect(offsets[:]))
         for q in range(QUADRANTS):
             nc.sync.dma_start(
-                out=x_scale[QUADRANT * q : QUADRANT * q + ROWS * PASSES, :].bitcast(I32),
-                in_=picked_scale[q:QUADRANT:QUADRANTS, :].bitcast(I32),
+                out=x_scale[QUADRANT * q : QUADRANT * q + ROWS, :].bitcast(I32),
+                in_=picked_scale[QUADRANT * q : QUADRANT * (q + 1) : step, :].bitcast(I32),
             )
-        word_table.append(load_words(1, "first"))
+        side_rows = [load_side(b) for b in range(BLOCKS)]
 
         halves = [offsets[:, h * HALF // GROUP : (h + 1) * HALF // GROUP] for h in range(2)]
 
         w_bf = [keep.tile([P, N, PACK], BF16, name=f"w_bf{g}", tag=f"bf{g}", align_bytes=64) for g in range(PASSES)]
-        nc.scalar.copy(out=w_bf[0][:], in_=w_raw[:, 0].rearrange("p j m -> p m j"))
-        nc.vector.tensor_copy(out=w_bf[1][:], in_=w_raw[:, 1].rearrange("p j m -> p m j"))
-        side_rows = [load_side(0, "side0")]
         w_codes = keep.tile([P, PASSES * N], U32, name="w_codes", align_bytes=64)
         w_scales = keep.tile([P, PASSES * N], U8, name="w_scales", align_bytes=64)
-        for g in reversed(range(PASSES)):
+        for g in range(PASSES):
+            nc.scalar.copy(out=w_bf[g][:], in_=w_raw[g][:].rearrange("p j m -> p m j"))
+        for g in range(PASSES):
             cols = slice(g * N, (g + 1) * N)
             nc.vector.quantize_mx(
                 out=w_codes[:, cols].bitcast(FP8X4), scales=w_scales[:, cols], in_=w_bf[g][:].rearrange("p m j -> p (m j)")
             )
-        side_rows.append(load_side(1, "bf1"))
 
         acc = [[psum.tile([P, HALF], F32, name=f"acc{b}{h}") for h in range(2)] for b in range(BLOCKS)]
 
+        x_codes = []
         for g in range(PASSES):
-            x_codes = keep.tile([P, S], U32, name=f"x_codes{g}", tag=("bf0", "words0")[g], align_bytes=64)
+            codes = keep.tile([P, S], U32, name=f"x_codes{g}", tag=("bf1", "words0")[g], align_bytes=64)
             for h in range(2):
-                entries = slice(h * HALF, (h + 1) * HALF)
-                nc.vector.tensor_copy(x_codes[:, entries], word_table[g][:].indirect(halves[h]))
-                for b in range(BLOCKS):
-                    cols = slice(g * N + b * P, g * N + (b + 1) * P)
+                nc.vector.tensor_copy(codes[:, h * HALF : (h + 1) * HALF], word_table[g][:].indirect(halves[h]))
+            x_codes.append(codes)
+        for b in range(BLOCKS):
+            for g in range(PASSES):
+                cols = slice(g * N + b * P, g * N + (b + 1) * P)
+                for h in range(2):
                     nc.tensor.matmul_mx(
                         out=acc[b][h][:],
                         lhsT=w_codes[:, cols].bitcast(FP8X4),
                         lhsT_scale=w_scales[:, cols],
-                        rhs=x_codes[:, entries].bitcast(FP8X4),
-                        rhs_scale=x_scale[ROWS * g : P, entries],
+                        rhs=x_codes[g][:, h * HALF : (h + 1) * HALF].bitcast(FP8X4),
+                        rhs_scale=x_scale[:, g * S + h * HALF : g * S + (h + 1) * HALF],
                         start=(g == 0),
                         stop=(g == PASSES - 1),
                     )
@@ -125,7 +133,7 @@ def tile_picked_sidegate_silu_p_kernel(tc, x_words, x_scales, side, w1, offs, ou
         for h in range(2):
             nc.vector.tensor_copy(y0[h], acc[0][h][:])
         parts0 = gate(0, y0)
-        y1_whole = keep.tile([P, S], F32, name="y1", tag="side0", align_bytes=64)
+        y1_whole = over.tile([P, S], F32, name="y1", offset=0, align_bytes=64)
         y1 = [y1_whole[:, h * HALF : (h + 1) * HALF] for h in range(2)]
         for h in range(2):
             nc.scalar.copy(out=y1[h], in_=acc[1][h][:])

@@ -37,11 +37,15 @@ def tile_picked_sidegate_silu_p_kernel(tc, x_words, x_scales, side, w1, offs, ou
         offsets = keep.tile([P, S // GROUP], U16, name="offsets")
 
         side_bytes = 4 * T
-        scale_table = over.tile([P, PASSES, T], U8, name="scale_table", offset=side_bytes - T, align_bytes=64)
-        nc.vector.memset(scale_table[:, 0, :].bitcast(I32), 0)
-        nc.gpsimd.memset(scale_table[:, 1, :].bitcast(I32), 0)
+        code_bytes = 4 * PASSES * N
+        scale_table = over.tile([P, PASSES, T], U8, name="scale_table", offset=side_bytes - T // 2, align_bytes=64)
+        nc.vector.memset(scale_table[:].rearrange("p g c -> p (g c)").bitcast(I32), 0)
         x_scale = keep.tile([P, PASSES * S], U8, name="x_scale", align_bytes=64)
         nc.gpsimd.memset(x_scale[:].bitcast(I32), 0)
+
+        warm = keep.tile([P, 2], F32, name="warm")
+        nc.gpsimd.memset(warm[:, 0:1], 0.0)
+        nc.scalar.activation(warm[:, 1:2], warm[:, 0:1], SIGMOID)
 
         def load_w(g):
             raw = keep.tile([P, PACK, N], F32, name=f"w_raw{g}", align_bytes=64)
@@ -54,7 +58,7 @@ def tile_picked_sidegate_silu_p_kernel(tc, x_words, x_scales, side, w1, offs, ou
             return table
 
         def load_side(b):
-            rows = over.tile([P, T], F32, name=f"side_rows{b}", offset=b * side_bytes, align_bytes=64)
+            rows = over.tile([P, T], F32, name=f"side_rows{b}", offset=b * (side_bytes + code_bytes), align_bytes=64)
             nc.sync.dma_start(out=rows[:], in_=side[b * P : (b + 1) * P, :])
             return rows
 
@@ -80,7 +84,7 @@ def tile_picked_sidegate_silu_p_kernel(tc, x_words, x_scales, side, w1, offs, ou
         halves = [offsets[:, h * HALF // GROUP : (h + 1) * HALF // GROUP] for h in range(2)]
 
         w_bf = [keep.tile([P, N, PACK], BF16, name=f"w_bf{g}", tag=f"bf{g}", align_bytes=64) for g in range(PASSES)]
-        w_codes = keep.tile([P, PASSES * N], U32, name="w_codes", align_bytes=64)
+        w_codes = over.tile([P, PASSES * N], U32, name="w_codes", offset=side_bytes, align_bytes=64)
         w_scales = keep.tile([P, PASSES * N], U8, name="w_scales", align_bytes=64)
         for g in range(PASSES):
             nc.scalar.copy(out=w_bf[g][:], in_=w_raw[g][:].rearrange("p j m -> p m j"))
@@ -99,9 +103,9 @@ def tile_picked_sidegate_silu_p_kernel(tc, x_words, x_scales, side, w1, offs, ou
                 nc.vector.tensor_copy(codes[:, h * HALF : (h + 1) * HALF], word_table[g][:].indirect(halves[h]))
             x_codes.append(codes)
         for b in range(BLOCKS):
-            for g in range(PASSES):
-                cols = slice(g * N + b * P, g * N + (b + 1) * P)
-                for h in range(2):
+            for h in range(2):
+                for g in range(PASSES):
+                    cols = slice(g * N + b * P, g * N + (b + 1) * P)
                     nc.tensor.matmul_mx(
                         out=acc[b][h][:],
                         lhsT=w_codes[:, cols].bitcast(FP8X4),

@@ -20,10 +20,14 @@ PACK = 4
 PASSES = K // (P * PACK)
 BLOCKS = N // P
 QUADRANT = 32
-QUADRANTS = P // QUADRANT
 ROWS = 4
+ROW_STEP = QUADRANT // ROWS
 GROUP = 16
 HALF = S // 2
+
+SIDE_BYTES = 4 * T
+CODE_BYTES = 4 * PASSES * N
+TABLE_OFFSET = SIDE_BYTES - (PASSES * T - CODE_BYTES) // 2
 
 
 def tile_picked_sidegate_silu_p_kernel(tc, x_words, x_scales, side, w1, offs, out):
@@ -31,25 +35,18 @@ def tile_picked_sidegate_silu_p_kernel(tc, x_words, x_scales, side, w1, offs, ou
     with ExitStack() as ctx:
         keep = ctx.enter_context(tc.tile_pool(name="keep", bufs=1))
         psum = ctx.enter_context(tc.psum_pool(name="psum", bufs=1))
-
-        over = ctx.enter_context(tc.tile_pool(name="over", bufs=1))
+        shared = ctx.enter_context(tc.tile_pool(name="shared", bufs=1))
 
         offsets = keep.tile([P, S // GROUP], U16, name="offsets")
 
-        side_bytes = 4 * T
-        code_bytes = 4 * PASSES * N
-        scale_table = over.tile([P, PASSES, T], U8, name="scale_table", offset=side_bytes - T // 2, align_bytes=64)
+        scale_table = shared.tile([P, PASSES, T], U8, name="scale_table", offset=TABLE_OFFSET, align_bytes=64)
         nc.vector.memset(scale_table[:].rearrange("p g c -> p (g c)").bitcast(I32), 0)
         x_scale = keep.tile([P, PASSES * S], U8, name="x_scale", align_bytes=64)
-        nc.gpsimd.memset(x_scale[:].bitcast(I32), 0)
-
-        warm = keep.tile([P, 2], F32, name="warm")
-        nc.gpsimd.memset(warm[:, 0:1], 0.0)
-        nc.scalar.activation(warm[:, 1:2], warm[:, 0:1], SIGMOID)
 
         def load_w(g):
             raw = keep.tile([P, PACK, N], F32, name=f"w_raw{g}", align_bytes=64)
-            nc.sync.dma_start(out=raw[:], in_=w1[g * P * PACK : (g + 1) * P * PACK, :].rearrange("(p j) m -> p j m", j=PACK))
+            rows = w1[g * P * PACK : (g + 1) * P * PACK, :]
+            nc.sync.dma_start(out=raw[:], in_=rows.rearrange("(p j) m -> p j m", j=PACK))
             return raw
 
         def load_words(g):
@@ -58,33 +55,32 @@ def tile_picked_sidegate_silu_p_kernel(tc, x_words, x_scales, side, w1, offs, ou
             return table
 
         def load_side(b):
-            rows = over.tile([P, T], F32, name=f"side_rows{b}", offset=b * (side_bytes + code_bytes), align_bytes=64)
+            rows = shared.tile([P, T], F32, name=f"side_rows{b}", offset=b * (SIDE_BYTES + CODE_BYTES), align_bytes=64)
             nc.sync.dma_start(out=rows[:], in_=side[b * P : (b + 1) * P, :])
             return rows
 
         w_raw = [load_w(0)]
-        step = QUADRANT // ROWS
-        nc.sync.dma_start(
-            out=scale_table[0:P:step].bitcast(I32), in_=x_scales.rearrange("g i c -> i g c").bitcast(I32)
-        )
         nc.sync.dma_start(offsets[:], offs)
+        nc.sync.dma_start(
+            out=scale_table[0:P:ROW_STEP].bitcast(I32), in_=x_scales.rearrange("g i c -> i g c").bitcast(I32)
+        )
         w_raw.append(load_w(1))
         word_table = [load_words(g) for g in range(PASSES)]
 
         picked_scale = keep.tile([P, PASSES * S], U8, name="picked_scale", align_bytes=64)
         for g in range(PASSES):
             nc.vector.tensor_copy(picked_scale[:, g * S : (g + 1) * S], scale_table[:, g, :].indirect(offsets[:]))
-        for q in range(QUADRANTS):
+        nc.vector.tensor_copy(x_scale[:].bitcast(I32), picked_scale[:].bitcast(I32))
+        for r in range(1, ROWS):
             nc.sync.dma_start(
-                out=x_scale[QUADRANT * q : QUADRANT * q + ROWS, :].bitcast(I32),
-                in_=picked_scale[QUADRANT * q : QUADRANT * (q + 1) : step, :].bitcast(I32),
+                out=x_scale[r:P:QUADRANT, :].bitcast(I32), in_=picked_scale[ROW_STEP * r : P : QUADRANT, :].bitcast(I32)
             )
         side_rows = [load_side(b) for b in range(BLOCKS)]
 
         halves = [offsets[:, h * HALF // GROUP : (h + 1) * HALF // GROUP] for h in range(2)]
 
         w_bf = [keep.tile([P, N, PACK], BF16, name=f"w_bf{g}", tag=f"bf{g}", align_bytes=64) for g in range(PASSES)]
-        w_codes = over.tile([P, PASSES * N], U32, name="w_codes", offset=side_bytes, align_bytes=64)
+        w_codes = shared.tile([P, PASSES * N], U32, name="w_codes", offset=SIDE_BYTES, align_bytes=64)
         w_scales = keep.tile([P, PASSES * N], U8, name="w_scales", align_bytes=64)
         for g in range(PASSES):
             nc.scalar.copy(out=w_bf[g][:], in_=w_raw[g][:].rearrange("p j m -> p m j"))
@@ -102,9 +98,9 @@ def tile_picked_sidegate_silu_p_kernel(tc, x_words, x_scales, side, w1, offs, ou
             for h in range(2):
                 nc.vector.tensor_copy(codes[:, h * HALF : (h + 1) * HALF], word_table[g][:].indirect(halves[h]))
             x_codes.append(codes)
-        for b in range(BLOCKS):
-            for h in range(2):
-                for g in range(PASSES):
+        for h in range(2):
+            for g in range(PASSES):
+                for b in range(BLOCKS):
                     cols = slice(g * N + b * P, g * N + (b + 1) * P)
                     nc.tensor.matmul_mx(
                         out=acc[b][h][:],
@@ -116,30 +112,37 @@ def tile_picked_sidegate_silu_p_kernel(tc, x_words, x_scales, side, w1, offs, ou
                         stop=(g == PASSES - 1),
                     )
 
-        def gate(b, y):
-            parts = []
-            for h in range(2):
-                picked = side_rows[b][:].indirect(halves[h])
-                sig = keep.tile([P, HALF], F32, name=f"sig{h}")
-                nc.scalar.activation(sig[:], picked, SIGMOID)
-                prod = keep.tile([P, HALF], F32, name=f"prod{h}")
-                nc.vector.tensor_tensor(prod[:], picked, y[h], MULT)
-                parts.append((sig, prod))
-            return parts
+        def picked_side(b, h):
+            return side_rows[b][:].indirect(halves[h])
 
-        def finish(b, parts):
-            for h, (sig, prod) in enumerate(parts):
-                res = keep.tile([P, HALF], F32, name=f"res{b}{h}")
-                nc.vector.tensor_tensor(res[:], prod[:], sig[:], MULT)
-                nc.sync.dma_start(out=out[b * P : (b + 1) * P, h * HALF : (h + 1) * HALF], in_=res[:])
+        def sigmoid(b, h):
+            sig = keep.tile([P, HALF], F32, name=f"sig{h}")
+            nc.scalar.activation(sig[:], picked_side(b, h), SIGMOID)
+            return sig
 
-        y0 = [keep.tile([P, HALF], F32, name=f"y0{h}")[:] for h in range(2)]
-        for h in range(2):
-            nc.vector.tensor_copy(y0[h], acc[0][h][:])
-        parts0 = gate(0, y0)
-        y1_whole = over.tile([P, S], F32, name="y1", offset=0, align_bytes=64)
-        y1 = [y1_whole[:, h * HALF : (h + 1) * HALF] for h in range(2)]
-        for h in range(2):
-            nc.scalar.copy(out=y1[h], in_=acc[1][h][:])
-        finish(0, parts0)
-        finish(1, gate(1, y1))
+        def times_side(b, h, factor):
+            prod = keep.tile([P, HALF], F32, name=f"prod{h}")
+            nc.vector.tensor_tensor(prod[:], picked_side(b, h), factor, MULT)
+            return prod
+
+        def finish(b, h, prod, factor):
+            res = keep.tile([P, HALF], F32, name=f"res{b}{h}")
+            nc.vector.tensor_tensor(res[:], prod[:], factor, MULT)
+            nc.sync.dma_start(out=out[b * P : (b + 1) * P, h * HALF : (h + 1) * HALF], in_=res[:])
+
+        y00 = keep.tile([P, HALF], F32, name="y00")
+        nc.vector.tensor_copy(y00[:], acc[0][0][:])
+        y10 = keep.tile([P, HALF], F32, name="y10")
+        nc.vector.tensor_copy(y10[:], acc[1][0][:])
+        sig01 = sigmoid(0, 1)
+        prod00 = times_side(0, 0, y00[:])
+        sig00 = sigmoid(0, 0)
+        prod01 = times_side(0, 1, sig01[:])
+        y11 = shared.tile([P, HALF], F32, name="y11", offset=0, align_bytes=64)
+        nc.scalar.copy(out=y11[:], in_=acc[1][1][:])
+        y1 = [y10[:], y11[:]]
+        finish(0, 0, prod00, sig00[:])
+        finish(0, 1, prod01, acc[0][1][:])
+        parts = [(sigmoid(1, h), times_side(1, h, y1[h])) for h in range(2)]
+        for h, (sig, prod) in enumerate(parts):
+            finish(1, h, prod, sig[:])

@@ -82,8 +82,12 @@ def tile_picked_sidegate_silu_p_kernel(tc, x_words, x_scales, side, w1, offs, ou
         w_bf = [keep.tile([P, N, PACK], BF16, name=f"w_bf{g}", tag=f"bf{g}", align_bytes=64) for g in range(PASSES)]
         w_codes = shared.tile([P, PASSES * N], U32, name="w_codes", offset=SIDE_BYTES, align_bytes=64)
         w_scales = keep.tile([P, PASSES * N], U8, name="w_scales", align_bytes=64)
+        warm = keep.tile([P, 1], F32, name="warm")
+        nc.scalar.activation(warm[:], w_raw[0][:, 0, 0:1], SIGMOID)
         for g in range(PASSES):
-            nc.scalar.copy(out=w_bf[g][:], in_=w_raw[g][:].rearrange("p j m -> p m j"))
+            for b in range(BLOCKS):
+                cols = slice(b * P, (b + 1) * P)
+                nc.scalar.copy(out=w_bf[g][:, cols, :], in_=w_raw[g][:, :, cols].rearrange("p j m -> p m j"))
         for g in range(PASSES):
             cols = slice(g * N, (g + 1) * N)
             nc.vector.quantize_mx(
@@ -131,9 +135,9 @@ def tile_picked_sidegate_silu_p_kernel(tc, x_words, x_scales, side, w1, offs, ou
             nc.sync.dma_start(out=out[b * P : (b + 1) * P, h * HALF : (h + 1) * HALF], in_=res[:])
 
         y00 = keep.tile([P, HALF], F32, name="y00")
-        nc.vector.tensor_copy(y00[:], acc[0][0][:])
+        nc.scalar.copy(out=y00[:], in_=acc[0][0][:])
         y10 = keep.tile([P, HALF], F32, name="y10")
-        nc.vector.tensor_copy(y10[:], acc[1][0][:])
+        nc.scalar.copy(out=y10[:], in_=acc[1][0][:])
         sig01 = sigmoid(0, 1)
         prod00 = times_side(0, 0, y00[:])
         sig00 = sigmoid(0, 0)

@@ -102,9 +102,9 @@ def tile_picked_sidegate_silu_p_kernel(tc, x_words, x_scales, side, w1, offs, ou
             for h in range(2):
                 nc.vector.tensor_copy(codes[:, h * HALF : (h + 1) * HALF], word_table[g][:].indirect(halves[h]))
             x_codes.append(codes)
-        for h in range(2):
+        for b in range(BLOCKS):
             for g in range(PASSES):
-                for b in range(BLOCKS):
+                for h in range(2):
                     cols = slice(g * N + b * P, g * N + (b + 1) * P)
                     nc.tensor.matmul_mx(
                         out=acc[b][h][:],
@@ -134,19 +134,10 @@ def tile_picked_sidegate_silu_p_kernel(tc, x_words, x_scales, side, w1, offs, ou
             nc.vector.tensor_tensor(res[:], prod[:], factor, MULT)
             nc.sync.dma_start(out=out[b * P : (b + 1) * P, h * HALF : (h + 1) * HALF], in_=res[:])
 
-        y00 = keep.tile([P, HALF], F32, name="y00")
-        nc.scalar.copy(out=y00[:], in_=acc[0][0][:])
-        y10 = keep.tile([P, HALF], F32, name="y10")
-        nc.scalar.copy(out=y10[:], in_=acc[1][0][:])
-        sig01 = sigmoid(0, 1)
-        prod00 = times_side(0, 0, y00[:])
-        sig00 = sigmoid(0, 0)
-        prod01 = times_side(0, 1, sig01[:])
-        y11 = shared.tile([P, HALF], F32, name="y11", offset=0, align_bytes=64)
-        nc.scalar.copy(out=y11[:], in_=acc[1][1][:])
-        y1 = [y10[:], y11[:]]
-        finish(0, 0, prod00, sig00[:])
-        finish(0, 1, prod01, acc[0][1][:])
-        parts = [(sigmoid(1, h), times_side(1, h, y1[h])) for h in range(2)]
-        for h, (sig, prod) in enumerate(parts):
-            finish(1, h, prod, sig[:])
+        for b in range(BLOCKS):
+            y = [keep.tile([P, HALF], F32, name=f"y{b}{h}", tag=f"y{h}") for h in range(2)]
+            for h in range(2):
+                nc.scalar.copy(out=y[h][:], in_=acc[b][h][:])
+            parts = [(sigmoid(b, h), times_side(b, h, y[h][:])) for h in range(2)]
+            for h, (sig, prod) in enumerate(parts):
+                finish(b, h, prod, sig[:])

@@ -12,7 +12,8 @@ U32 = mybir.dt.uint32
 U16 = mybir.dt.uint16
 U8 = mybir.dt.uint8
 FP8X4 = mybir.dt.float8_e4m3fn_x4
-SIGMOID = mybir.ActivationFunctionType.Sigmoid
+SILU = mybir.ActivationFunctionType.Silu
+COPY = mybir.ActivationFunctionType.Copy
 MULT = mybir.AluOpType.mult
 
 P = 128
@@ -23,7 +24,9 @@ QUADRANT = 32
 ROWS = 4
 ROW_STEP = QUADRANT // ROWS
 GROUP = 16
-HALF = S // 2
+GATHER_CUTS = (0, 64, 192, 320, S)
+PIECE_CUTS = (0, 64, 192, 320, 416, S)
+STORE_CUTS = (0, 192, 320, S)
 
 SIDE_BYTES = 4 * T
 CODE_BYTES = 4 * PASSES * N
@@ -77,13 +80,11 @@ def tile_picked_sidegate_silu_p_kernel(tc, x_words, x_scales, side, w1, offs, ou
             )
         side_rows = [load_side(b) for b in range(BLOCKS)]
 
-        halves = [offsets[:, h * HALF // GROUP : (h + 1) * HALF // GROUP] for h in range(2)]
-
         w_bf = [keep.tile([P, N, PACK], BF16, name=f"w_bf{g}", tag=f"bf{g}", align_bytes=64) for g in range(PASSES)]
         w_codes = shared.tile([P, PASSES * N], U32, name="w_codes", offset=SIDE_BYTES, align_bytes=64)
         w_scales = keep.tile([P, PASSES * N], U8, name="w_scales", align_bytes=64)
         warm = keep.tile([P, 1], F32, name="warm")
-        nc.scalar.activation(warm[:], w_raw[0][:, 0, 0:1], SIGMOID)
+        nc.scalar.activation(warm[:], w_raw[0][:, 0, 0:1], SILU)
         for g in range(PASSES):
             for b in range(BLOCKS):
                 cols = slice(b * P, (b + 1) * P)
@@ -94,50 +95,42 @@ def tile_picked_sidegate_silu_p_kernel(tc, x_words, x_scales, side, w1, offs, ou
                 out=w_codes[:, cols].bitcast(FP8X4), scales=w_scales[:, cols], in_=w_bf[g][:].rearrange("p m j -> p (m j)")
             )
 
-        acc = [[psum.tile([P, HALF], F32, name=f"acc{b}{h}") for h in range(2)] for b in range(BLOCKS)]
+        acc = [psum.tile([P, S], F32, name=f"acc{b}") for b in range(BLOCKS)]
 
         x_codes = []
         for g in range(PASSES):
             codes = keep.tile([P, S], U32, name=f"x_codes{g}", tag=("bf1", "words0")[g], align_bytes=64)
-            for h in range(2):
-                nc.vector.tensor_copy(codes[:, h * HALF : (h + 1) * HALF], word_table[g][:].indirect(halves[h]))
+            nc.vector.tensor_copy(codes[:], word_table[g][:].indirect(offsets[:]))
             x_codes.append(codes)
-        for b in range(BLOCKS):
-            for g in range(PASSES):
-                for h in range(2):
-                    cols = slice(g * N + b * P, g * N + (b + 1) * P)
-                    nc.tensor.matmul_mx(
-                        out=acc[b][h][:],
-                        lhsT=w_codes[:, cols].bitcast(FP8X4),
-                        lhsT_scale=w_scales[:, cols],
-                        rhs=x_codes[g][:, h * HALF : (h + 1) * HALF].bitcast(FP8X4),
-                        rhs_scale=x_scale[:, g * S + h * HALF : g * S + (h + 1) * HALF],
-                        start=(g == 0),
-                        stop=(g == PASSES - 1),
-                    )
+        for g in range(PASSES):
+            for b in range(BLOCKS):
+                cols = slice(g * N + b * P, g * N + (b + 1) * P)
+                nc.tensor.matmul_mx(
+                    out=acc[b][:],
+                    lhsT=w_codes[:, cols].bitcast(FP8X4),
+                    lhsT_scale=w_scales[:, cols],
+                    rhs=x_codes[g][:].bitcast(FP8X4),
+                    rhs_scale=x_scale[:, g * S : (g + 1) * S],
+                    start=(g == 0),
+                    stop=(g == PASSES - 1),
+                )
 
-        def picked_side(b, h):
-            return side_rows[b][:].indirect(halves[h])
-
-        def sigmoid(b, h):
-            sig = keep.tile([P, HALF], F32, name=f"sig{h}")
-            nc.scalar.activation(sig[:], picked_side(b, h), SIGMOID)
-            return sig
-
-        def times_side(b, h, factor):
-            prod = keep.tile([P, HALF], F32, name=f"prod{h}")
-            nc.vector.tensor_tensor(prod[:], picked_side(b, h), factor, MULT)
-            return prod
-
-        def finish(b, h, prod, factor):
-            res = keep.tile([P, HALF], F32, name=f"res{b}{h}")
-            nc.vector.tensor_tensor(res[:], prod[:], factor, MULT)
-            nc.sync.dma_start(out=out[b * P : (b + 1) * P, h * HALF : (h + 1) * HALF], in_=res[:])
+        def stretches(cuts):
+            return list(zip(cuts[:-1], cuts[1:]))
 
         for b in range(BLOCKS):
-            y = [keep.tile([P, HALF], F32, name=f"y{b}{h}", tag=f"y{h}") for h in range(2)]
-            for h in range(2):
-                nc.scalar.copy(out=y[h][:], in_=acc[b][h][:])
-            parts = [(sigmoid(b, h), times_side(b, h, y[h][:])) for h in range(2)]
-            for h, (sig, prod) in enumerate(parts):
-                finish(b, h, prod, sig[:])
+            picked = keep.tile([P, S], F32, name=f"picked{b}")
+            gate = keep.tile([P, S], F32, name=f"gate{b}")
+            res = keep.tile([P, S], F32, name=f"res{b}")
+            for i, (lo, hi) in enumerate(stretches(GATHER_CUTS)):
+                looked_up = side_rows[b][:].indirect(offsets[:, lo // GROUP : hi // GROUP])
+                if i % 2 == 0:
+                    nc.scalar.activation(picked[:, lo:hi], looked_up, COPY)
+                else:
+                    nc.vector.tensor_copy(picked[:, lo:hi], looked_up)
+            for lo, hi in stretches(PIECE_CUTS):
+                nc.scalar.activation(gate[:, lo:hi], picked[:, lo:hi], SILU)
+            for lo, hi in stretches(PIECE_CUTS):
+                nc.vector.tensor_tensor(res[:, lo:hi], gate[:, lo:hi], acc[b][:, lo:hi], MULT)
+            for lo, hi in stretches(STORE_CUTS if b == BLOCKS - 1 else (0, S)):
+                nc.sync.dma_start(out=out[b * P : (b + 1) * P, lo:hi], in_=res[:, lo:hi])

@@ -25,8 +25,8 @@ ROWS = 4
 ROW_STEP = QUADRANT // ROWS
 GROUP = 16
 GATHER_CUTS = (0, 64, 192, 320, S)
-PIECE_CUTS = (0, 64, 192, 320, 416, S)
-STORE_CUTS = (0, 192, 320, S)
+PIECE_CUTS = (0, 64, 128, 192, 256, 320, 384, 448, S)
+STORE_CUTS = (0, 128, 320, S)
 
 SIDE_BYTES = 4 * T
 CODE_BYTES = 4 * PASSES * N

@@ -24,7 +24,7 @@ QUADRANT = 32
 ROWS = 4
 ROW_STEP = QUADRANT // ROWS
 GROUP = 16
-GATHER_CUTS = (0, 64, 192, 320, S)
+GATHER_CUTS = (0, 64, 192, 320, 448, S)
 PIECE_CUTS = (0, 64, 128, 192, 256, 320, 384, 448, S)
 STORE_CUTS = (0, 128, 320, S)
 
@@ -115,6 +115,9 @@ def tile_picked_sidegate_silu_p_kernel(tc, x_words, x_scales, side, w1, offs, ou
                     stop=(g == PASSES - 1),
                 )
 
+        ones = keep.tile([P, 64], F32, name="ones")
+        nc.vector.memset(ones[:], 1.0)
+
         def stretches(cuts):
             return list(zip(cuts[:-1], cuts[1:]))
 
@@ -124,8 +127,10 @@ def tile_picked_sidegate_silu_p_kernel(tc, x_words, x_scales, side, w1, offs, ou
             res = keep.tile([P, S], F32, name=f"res{b}")
             for i, (lo, hi) in enumerate(stretches(GATHER_CUTS)):
                 looked_up = side_rows[b][:].indirect(offsets[:, lo // GROUP : hi // GROUP])
-                if i % 2 == 0:
+                if i in (0, 2):
                     nc.scalar.activation(picked[:, lo:hi], looked_up, COPY)
+                elif hi == S:
+                    nc.vector.tensor_tensor(picked[:, lo:hi], looked_up, ones[:], MULT)
                 else:
                     nc.vector.tensor_copy(picked[:, lo:hi], looked_up)
             for lo, hi in stretches(PIECE_CUTS):

@@ -22,7 +22,8 @@ PASSES = K // (P * PACK)
 BLOCKS = N // P
 QUADRANT = 32
 ROWS = 4
-ROW_STEP = QUADRANT // ROWS
+ROW_START = 32
+ROW_STEP = 4
 GROUP = 16
 GATHER_CUTS = (0, 64, 192, 320, 448, S)
 PIECE_CUTS = (0, 64, 128, 192, 256, 320, 384, 448, S)
@@ -45,6 +46,7 @@ def tile_picked_sidegate_silu_p_kernel(tc, x_words, x_scales, side, w1, offs, ou
         scale_table = shared.tile([P, PASSES, T], U8, name="scale_table", offset=TABLE_OFFSET, align_bytes=64)
         nc.vector.memset(scale_table[:].rearrange("p g c -> p (g c)").bitcast(I32), 0)
         x_scale = keep.tile([P, PASSES * S], U8, name="x_scale", align_bytes=64)
+        nc.vector.memset(x_scale[:].bitcast(I32), 0)
 
         def load_w(g):
             raw = keep.tile([P, PACK, N], F32, name=f"w_raw{g}", align_bytes=64)
@@ -64,8 +66,10 @@ def tile_picked_sidegate_silu_p_kernel(tc, x_words, x_scales, side, w1, offs, ou
 
         w_raw = [load_w(0)]
         nc.sync.dma_start(offsets[:], offs)
+        row_end = ROW_START + ROW_STEP * ROWS * ROWS
         nc.sync.dma_start(
-            out=scale_table[0:P:ROW_STEP].bitcast(I32), in_=x_scales.rearrange("g i c -> i g c").bitcast(I32)
+            out=scale_table[ROW_START:row_end:ROW_STEP].bitcast(I32),
+            in_=x_scales.rearrange("g i c -> i g c").bitcast(I32),
         )
         w_raw.append(load_w(1))
         word_table = [load_words(g) for g in range(PASSES)]
@@ -73,10 +77,10 @@ def tile_picked_sidegate_silu_p_kernel(tc, x_words, x_scales, side, w1, offs, ou
         picked_scale = keep.tile([P, PASSES * S], U8, name="picked_scale", align_bytes=64)
         for g in range(PASSES):
             nc.vector.tensor_copy(picked_scale[:, g * S : (g + 1) * S], scale_table[:, g, :].indirect(offsets[:]))
-        nc.vector.tensor_copy(x_scale[:].bitcast(I32), picked_scale[:].bitcast(I32))
-        for r in range(1, ROWS):
+        for r in range(ROWS):
             nc.sync.dma_start(
-                out=x_scale[r:P:QUADRANT, :].bitcast(I32), in_=picked_scale[ROW_STEP * r : P : QUADRANT, :].bitcast(I32)
+                out=x_scale[r:P:QUADRANT, :].bitcast(I32),
+                in_=picked_scale[ROW_START + ROW_STEP * r : row_end : ROW_STEP * ROWS, :].bitcast(I32),
             )
         side_rows = [load_side(b) for b in range(BLOCKS)]
 

@@ -24,6 +24,7 @@ QUADRANT = 32
 ROWS = 4
 ROW_START = 32
 ROW_STEP = 4
+ALIGN = 256
 GROUP = 16
 GATHER_CUTS = (0, 64, 192, 320, 448, S)
 PIECE_CUTS = (0, 64, 128, 192, 256, 320, 384, 448, S)
@@ -41,26 +42,26 @@ def tile_picked_sidegate_silu_p_kernel(tc, x_words, x_scales, side, w1, offs, ou
         psum = ctx.enter_context(tc.psum_pool(name="psum", bufs=1))
         shared = ctx.enter_context(tc.tile_pool(name="shared", bufs=1))
 
-        offsets = keep.tile([P, S // GROUP], U16, name="offsets")
+        offsets = keep.tile([P, S // GROUP], U16, name="offsets", align_bytes=ALIGN)
 
-        scale_table = shared.tile([P, PASSES, T], U8, name="scale_table", offset=TABLE_OFFSET, align_bytes=64)
+        scale_table = shared.tile([P, PASSES, T], U8, name="scale_table", offset=TABLE_OFFSET, align_bytes=ALIGN)
         nc.vector.memset(scale_table[:].rearrange("p g c -> p (g c)").bitcast(I32), 0)
-        x_scale = keep.tile([P, PASSES * S], U8, name="x_scale", align_bytes=64)
+        x_scale = keep.tile([P, PASSES * S], U8, name="x_scale", align_bytes=ALIGN)
         nc.vector.memset(x_scale[:].bitcast(I32), 0)
 
         def load_w(g):
-            raw = keep.tile([P, PACK, N], F32, name=f"w_raw{g}", align_bytes=64)
+            raw = keep.tile([P, PACK, N], F32, name=f"w_raw{g}", align_bytes=ALIGN)
             rows = w1[g * P * PACK : (g + 1) * P * PACK, :]
             nc.sync.dma_start(out=raw[:], in_=rows.rearrange("(p j) m -> p j m", j=PACK))
             return raw
 
         def load_words(g):
-            table = keep.tile([P, T], U32, name=f"word_table{g}", tag=f"words{g}", align_bytes=64)
+            table = keep.tile([P, T], U32, name=f"word_table{g}", tag=f"words{g}", align_bytes=ALIGN)
             nc.sync.dma_start(out=table[:].bitcast(I32), in_=x_words[g].rearrange("p n t -> p (n t)").bitcast(I32))
             return table
 
         def load_side(b):
-            rows = shared.tile([P, T], F32, name=f"side_rows{b}", offset=b * (SIDE_BYTES + CODE_BYTES), align_bytes=64)
+            rows = shared.tile([P, T], F32, name=f"side_rows{b}", offset=b * (SIDE_BYTES + CODE_BYTES), align_bytes=ALIGN)
             nc.sync.dma_start(out=rows[:], in_=side[b * P : (b + 1) * P, :])
             return rows
 
@@ -74,7 +75,7 @@ def tile_picked_sidegate_silu_p_kernel(tc, x_words, x_scales, side, w1, offs, ou
         w_raw.append(load_w(1))
         word_table = [load_words(g) for g in range(PASSES)]
 
-        picked_scale = keep.tile([P, PASSES * S], U8, name="picked_scale", align_bytes=64)
+        picked_scale = keep.tile([P, PASSES * S], U8, name="picked_scale", align_bytes=ALIGN)
         for g in range(PASSES):
             nc.vector.tensor_copy(picked_scale[:, g * S : (g + 1) * S], scale_table[:, g, :].indirect(offsets[:]))
         for r in range(ROWS):
@@ -84,9 +85,9 @@ def tile_picked_sidegate_silu_p_kernel(tc, x_words, x_scales, side, w1, offs, ou
             )
         side_rows = [load_side(b) for b in range(BLOCKS)]
 
-        w_bf = [keep.tile([P, N, PACK], BF16, name=f"w_bf{g}", tag=f"bf{g}", align_bytes=64) for g in range(PASSES)]
-        w_codes = shared.tile([P, PASSES * N], U32, name="w_codes", offset=SIDE_BYTES, align_bytes=64)
-        w_scales = keep.tile([P, PASSES * N], U8, name="w_scales", align_bytes=64)
+        w_bf = [keep.tile([P, N, PACK], BF16, name=f"w_bf{g}", tag=f"bf{g}", align_bytes=ALIGN) for g in range(PASSES)]
+        w_codes = shared.tile([P, PASSES * N], U32, name="w_codes", offset=SIDE_BYTES, align_bytes=ALIGN)
+        w_scales = keep.tile([P, PASSES * N], U8, name="w_scales", align_bytes=ALIGN)
         warm = keep.tile([P, 1], F32, name="warm")
         nc.scalar.activation(warm[:], w_raw[0][:, 0, 0:1], SILU)
         for g in range(PASSES):
@@ -103,7 +104,7 @@ def tile_picked_sidegate_silu_p_kernel(tc, x_words, x_scales, side, w1, offs, ou
 
         x_codes = []
         for g in range(PASSES):
-            codes = keep.tile([P, S], U32, name=f"x_codes{g}", tag=("bf1", "words0")[g], align_bytes=64)
+            codes = keep.tile([P, S], U32, name=f"x_codes{g}", tag=("bf1", "words0")[g], align_bytes=ALIGN)
             nc.vector.tensor_copy(codes[:], word_table[g][:].indirect(offsets[:]))
             x_codes.append(codes)
         for g in range(PASSES):
@@ -128,7 +129,7 @@ def tile_picked_sidegate_silu_p_kernel(tc, x_words, x_scales, side, w1, offs, ou
         for b in range(BLOCKS):
             picked = keep.tile([P, S], F32, name=f"picked{b}")
             gate = keep.tile([P, S], F32, name=f"gate{b}")
-            res = keep.tile([P, S], F32, name=f"res{b}")
+            res = keep.tile([P, S], F32, name=f"res{b}", align_bytes=ALIGN)
             for i, (lo, hi) in enumerate(stretches(GATHER_CUTS)):
                 looked_up = side_rows[b][:].indirect(offsets[:, lo // GROUP : hi // GROUP])
                 if i in (0, 2):

@@ -25,6 +25,7 @@ ROWS = 4
 ROW_START = 32
 ROW_STEP = 4
 ALIGN = 256
+HALF = S // 2
 GROUP = 16
 GATHER_CUTS = (0, 64, 192, 320, 448, S)
 PIECE_CUTS = (0, 64, 128, 192, 256, 320, 384, 448, S)
@@ -55,11 +56,6 @@ def tile_picked_sidegate_silu_p_kernel(tc, x_words, x_scales, side, w1, offs, ou
             nc.sync.dma_start(out=raw[:], in_=rows.rearrange("(p j) m -> p j m", j=PACK))
             return raw
 
-        def load_words(g):
-            table = keep.tile([P, T], U32, name=f"word_table{g}", tag=f"words{g}", align_bytes=ALIGN)
-            nc.sync.dma_start(out=table[:].bitcast(I32), in_=x_words[g].rearrange("p n t -> p (n t)").bitcast(I32))
-            return table
-
         def load_side(b):
             rows = shared.tile([P, T], F32, name=f"side_rows{b}", offset=b * (SIDE_BYTES + CODE_BYTES), align_bytes=ALIGN)
             nc.sync.dma_start(out=rows[:], in_=side[b * P : (b + 1) * P, :])
@@ -73,7 +69,8 @@ def tile_picked_sidegate_silu_p_kernel(tc, x_words, x_scales, side, w1, offs, ou
             in_=x_scales.rearrange("g i c -> i g c").bitcast(I32),
         )
         w_raw.append(load_w(1))
-        word_table = [load_words(g) for g in range(PASSES)]
+        word_table = keep.tile([P, PASSES, T], U32, name="word_table", align_bytes=ALIGN)
+        nc.sync.dma_start(out=word_table[:].bitcast(I32), in_=x_words.rearrange("g p n t -> p g (n t)").bitcast(I32))
 
         picked_scale = keep.tile([P, PASSES * S], U8, name="picked_scale", align_bytes=ALIGN)
         for g in range(PASSES):
@@ -100,25 +97,28 @@ def tile_picked_sidegate_silu_p_kernel(tc, x_words, x_scales, side, w1, offs, ou
                 out=w_codes[:, cols].bitcast(FP8X4), scales=w_scales[:, cols], in_=w_bf[g][:].rearrange("p m j -> p (m j)")
             )
 
-        acc = [psum.tile([P, S], F32, name=f"acc{b}") for b in range(BLOCKS)]
+        acc = [[psum.tile([P, HALF], F32, name=f"acc{b}_{h}") for h in range(S // HALF)] for b in range(BLOCKS)]
 
-        x_codes = []
-        for g in range(PASSES):
-            codes = keep.tile([P, S], U32, name=f"x_codes{g}", tag=("bf1", "words0")[g], align_bytes=ALIGN)
-            nc.vector.tensor_copy(codes[:], word_table[g][:].indirect(offsets[:]))
-            x_codes.append(codes)
-        for g in range(PASSES):
+        for h in range(S // HALF):
+            x_codes = []
+            for g in range(PASSES):
+                tag = "bf1" if h == g == 0 else f"x_codes{g}_{h}"
+                codes = keep.tile([P, HALF], U32, name=f"x_codes{g}_{h}", tag=tag, align_bytes=ALIGN)
+                entries = offsets[:, h * HALF // GROUP : (h + 1) * HALF // GROUP]
+                nc.vector.tensor_copy(codes[:], word_table[:, g, :].indirect(entries))
+                x_codes.append(codes)
             for b in range(BLOCKS):
-                cols = slice(g * N + b * P, g * N + (b + 1) * P)
-                nc.tensor.matmul_mx(
-                    out=acc[b][:],
-                    lhsT=w_codes[:, cols].bitcast(FP8X4),
-                    lhsT_scale=w_scales[:, cols],
-                    rhs=x_codes[g][:].bitcast(FP8X4),
-                    rhs_scale=x_scale[:, g * S : (g + 1) * S],
-                    start=(g == 0),
-                    stop=(g == PASSES - 1),
-                )
+                for g in range(PASSES):
+                    cols = slice(g * N + b * P, g * N + (b + 1) * P)
+                    nc.tensor.matmul_mx(
+                        out=acc[b][h][:],
+                        lhsT=w_codes[:, cols].bitcast(FP8X4),
+                        lhsT_scale=w_scales[:, cols],
+                        rhs=x_codes[g][:].bitcast(FP8X4),
+                        rhs_scale=x_scale[:, g * S + h * HALF : g * S + (h + 1) * HALF],
+                        start=(g == 0),
+                        stop=(g == PASSES - 1),
+                    )
 
         ones = keep.tile([P, 64], F32, name="ones")
         nc.vector.memset(ones[:], 1.0)
@@ -141,6 +141,6 @@ def tile_picked_sidegate_silu_p_kernel(tc, x_words, x_scales, side, w1, offs, ou
             for lo, hi in stretches(PIECE_CUTS):
                 nc.scalar.activation(gate[:, lo:hi], picked[:, lo:hi], SILU)
             for lo, hi in stretches(PIECE_CUTS):
-                nc.vector.tensor_tensor(res[:, lo:hi], gate[:, lo:hi], acc[b][:, lo:hi], MULT)
+                nc.vector.tensor_tensor(res[:, lo:hi], gate[:, lo:hi], acc[b][lo // HALF][:, lo % HALF : lo % HALF + hi - lo], MULT)
             for lo, hi in stretches(STORE_CUTS if b == BLOCKS - 1 else (0, S)):
                 nc.sync.dma_start(out=out[b * P : (b + 1) * P, lo:hi], in_=res[:, lo:hi])

@@ -56,6 +56,11 @@ def tile_picked_sidegate_silu_p_kernel(tc, x_words, x_scales, side, w1, offs, ou
             nc.sync.dma_start(out=raw[:], in_=rows.rearrange("(p j) m -> p j m", j=PACK))
             return raw
 
+        def load_words(g):
+            table = keep.tile([P, T], U32, name=f"word_table{g}", align_bytes=ALIGN)
+            nc.sync.dma_start(out=table[:].bitcast(I32), in_=x_words[g].rearrange("p n t -> p (n t)").bitcast(I32))
+            return table
+
         def load_side(b):
             rows = shared.tile([P, T], F32, name=f"side_rows{b}", offset=b * (SIDE_BYTES + CODE_BYTES), align_bytes=ALIGN)
             nc.sync.dma_start(out=rows[:], in_=side[b * P : (b + 1) * P, :])
@@ -69,8 +74,7 @@ def tile_picked_sidegate_silu_p_kernel(tc, x_words, x_scales, side, w1, offs, ou
             in_=x_scales.rearrange("g i c -> i g c").bitcast(I32),
         )
         w_raw.append(load_w(1))
-        word_table = keep.tile([P, PASSES, T], U32, name="word_table", align_bytes=ALIGN)
-        nc.sync.dma_start(out=word_table[:].bitcast(I32), in_=x_words.rearrange("g p n t -> p g (n t)").bitcast(I32))
+        word_table = [load_words(g) for g in range(PASSES)]
 
         picked_scale = keep.tile([P, PASSES * S], U8, name="picked_scale", align_bytes=ALIGN)
         for g in range(PASSES):
@@ -99,22 +103,21 @@ def tile_picked_sidegate_silu_p_kernel(tc, x_words, x_scales, side, w1, offs, ou
 
         acc = [[psum.tile([P, HALF], F32, name=f"acc{b}_{h}") for h in range(S // HALF)] for b in range(BLOCKS)]
 
+        codes0 = keep.tile([P, S], U32, name="x_codes0", tag="bf1", align_bytes=ALIGN)
+        nc.vector.tensor_copy(codes0[:], word_table[0][:].indirect(offsets[:]))
+        codes1 = keep.tile([P, S], U32, name="x_codes1", align_bytes=ALIGN)
         for h in range(S // HALF):
-            x_codes = []
-            for g in range(PASSES):
-                tag = "bf1" if h == g == 0 else f"x_codes{g}_{h}"
-                codes = keep.tile([P, HALF], U32, name=f"x_codes{g}_{h}", tag=tag, align_bytes=ALIGN)
-                entries = offsets[:, h * HALF // GROUP : (h + 1) * HALF // GROUP]
-                nc.vector.tensor_copy(codes[:], word_table[:, g, :].indirect(entries))
-                x_codes.append(codes)
-            for b in range(BLOCKS):
-                for g in range(PASSES):
+            entries = offsets[:, h * HALF // GROUP : (h + 1) * HALF // GROUP]
+            nc.vector.tensor_copy(codes1[:, h * HALF : (h + 1) * HALF], word_table[1][:].indirect(entries))
+        for b in range(BLOCKS):
+            for g, codes in enumerate((codes0, codes1)):
+                for h in range(S // HALF):
                     cols = slice(g * N + b * P, g * N + (b + 1) * P)
                     nc.tensor.matmul_mx(
                         out=acc[b][h][:],
                         lhsT=w_codes[:, cols].bitcast(FP8X4),
                         lhsT_scale=w_scales[:, cols],
-                        rhs=x_codes[g][:].bitcast(FP8X4),
+                        rhs=codes[:, h * HALF : (h + 1) * HALF].bitcast(FP8X4),
                         rhs_scale=x_scale[:, g * S + h * HALF : g * S + (h + 1) * HALF],
                         start=(g == 0),
                         stop=(g == PASSES - 1),

@@ -63,7 +63,7 @@ def tile_picked_sidegate_silu_p_kernel(tc, x_words, x_scales, side, w1, offs, ou
 
         def load_side(b):
             rows = shared.tile([P, T], F32, name=f"side_rows{b}", offset=b * (SIDE_BYTES + CODE_BYTES), align_bytes=ALIGN)
-            nc.sync.dma_start(out=rows[:], in_=side[b * P : (b + 1) * P, :])
+            nc.sync.dma_start(out=rows[:], in_=side[b:N:BLOCKS, :])
             return rows
 
         w_raw = [load_w(0)]
@@ -94,7 +94,7 @@ def tile_picked_sidegate_silu_p_kernel(tc, x_words, x_scales, side, w1, offs, ou
         for g in range(PASSES):
             for b in range(BLOCKS):
                 cols = slice(b * P, (b + 1) * P)
-                nc.scalar.copy(out=w_bf[g][:, cols, :], in_=w_raw[g][:, :, cols].rearrange("p j m -> p m j"))
+                nc.scalar.copy(out=w_bf[g][:, cols, :], in_=w_raw[g][:, :, b:N:BLOCKS].rearrange("p j m -> p m j"))
         for g in range(PASSES):
             cols = slice(g * N, (g + 1) * N)
             nc.vector.quantize_mx(
@@ -146,4 +146,4 @@ def tile_picked_sidegate_silu_p_kernel(tc, x_words, x_scales, side, w1, offs, ou
             for lo, hi in stretches(PIECE_CUTS):
                 nc.vector.tensor_tensor(res[:, lo:hi], gate[:, lo:hi], acc[b][lo // HALF][:, lo % HALF : lo % HALF + hi - lo], MULT)
             for lo, hi in stretches(STORE_CUTS if b == BLOCKS - 1 else (0, S)):
-                nc.sync.dma_start(out=out[b * P : (b + 1) * P, lo:hi], in_=res[:, lo:hi])
+                nc.sync.dma_start(out=out[b:N:BLOCKS, lo:hi], in_=res[:, lo:hi])

from contextlib import ExitStack

import concourse.mybir as mybir

K, T, S, N = 1024, 2048, 512, 256
FLOPS = 2 * K * N * S

F32 = mybir.dt.float32
BF16 = mybir.dt.bfloat16
I32 = mybir.dt.int32
U32 = mybir.dt.uint32
U16 = mybir.dt.uint16
U8 = mybir.dt.uint8
FP8X4 = mybir.dt.float8_e4m3fn_x4
SILU = mybir.ActivationFunctionType.Silu
COPY = mybir.ActivationFunctionType.Copy
MULT = mybir.AluOpType.mult

P = 128
PACK = 4
PASSES = K // (P * PACK)
BLOCKS = N // P
QUADRANT = 32
ROWS = 4
ROW_START = 32
ROW_STEP = 4
ALIGN = 256
HALF = S // 2
GROUP = 16
GATHER_CUTS = (0, 64, 192, 320, 448, S)
PIECE_CUTS = (0, 64, 128, 192, 256, 320, 384, 448, S)
STORE_CUTS = (0, 128, 320, S)

SIDE_BYTES = 4 * T
CODE_BYTES = 4 * PASSES * N
TABLE_OFFSET = SIDE_BYTES - (PASSES * T - CODE_BYTES) // 2


def tile_picked_sidegate_silu_p_kernel(tc, x_words, x_scales, side, w1, offs, out):
    nc = tc.nc
    with ExitStack() as ctx:
        keep = ctx.enter_context(tc.tile_pool(name="keep", bufs=1))
        psum = ctx.enter_context(tc.psum_pool(name="psum", bufs=1))
        shared = ctx.enter_context(tc.tile_pool(name="shared", bufs=1))

        offsets = keep.tile([P, S // GROUP], U16, name="offsets", align_bytes=ALIGN)

        scale_table = shared.tile([P, PASSES, T], U8, name="scale_table", offset=TABLE_OFFSET, align_bytes=ALIGN)
        nc.vector.memset(scale_table[:].rearrange("p g c -> p (g c)").bitcast(I32), 0)
        x_scale = keep.tile([P, PASSES * S], U8, name="x_scale", align_bytes=ALIGN)
        nc.vector.memset(x_scale[:].bitcast(I32), 0)

        def load_w(g):
            raw = keep.tile([P, PACK, N], F32, name=f"w_raw{g}", align_bytes=ALIGN)
            rows = w1[g * P * PACK : (g + 1) * P * PACK, :]
            nc.sync.dma_start(out=raw[:], in_=rows.rearrange("(p j) m -> p j m", j=PACK))
            return raw

        def load_words(g):
            table = keep.tile([P, T], U32, name=f"word_table{g}", align_bytes=ALIGN)
            nc.sync.dma_start(out=table[:].bitcast(I32), in_=x_words[g].rearrange("p n t -> p (n t)").bitcast(I32))
            return table

        def load_side(b):
            rows = shared.tile([P, T], F32, name=f"side_rows{b}", offset=b * (SIDE_BYTES + CODE_BYTES), align_bytes=ALIGN)
            nc.sync.dma_start(out=rows[:], in_=side[b:N:BLOCKS, :])
            return rows

        w_raw = [load_w(0)]
        nc.sync.dma_start(offsets[:], offs)
        row_end = ROW_START + ROW_STEP * ROWS * ROWS
        nc.sync.dma_start(
            out=scale_table[ROW_START:row_end:ROW_STEP].bitcast(I32),
            in_=x_scales.rearrange("g i c -> i g c").bitcast(I32),
        )
        w_raw.append(load_w(1))
        word_table = [load_words(g) for g in range(PASSES)]

        picked_scale = keep.tile([P, PASSES * S], U8, name="picked_scale", align_bytes=ALIGN)
        for g in range(PASSES):
            nc.vector.tensor_copy(picked_scale[:, g * S : (g + 1) * S], scale_table[:, g, :].indirect(offsets[:]))
        for r in range(ROWS):
            nc.sync.dma_start(
                out=x_scale[r:P:QUADRANT, :].bitcast(I32),
                in_=picked_scale[ROW_START + ROW_STEP * r : row_end : ROW_STEP * ROWS, :].bitcast(I32),
            )
        side_rows = [load_side(b) for b in range(BLOCKS)]

        w_bf = [keep.tile([P, N, PACK], BF16, name=f"w_bf{g}", tag=f"bf{g}", align_bytes=ALIGN) for g in range(PASSES)]
        w_codes = shared.tile([P, PASSES * N], U32, name="w_codes", offset=SIDE_BYTES, align_bytes=ALIGN)
        w_scales = keep.tile([P, PASSES * N], U8, name="w_scales", align_bytes=ALIGN)
        warm = keep.tile([P, 1], F32, name="warm")
        nc.scalar.activation(warm[:], w_raw[0][:, 0, 0:1], SILU)
        for g in range(PASSES):
            for b in range(BLOCKS):
                cols = slice(b * P, (b + 1) * P)
                nc.scalar.copy(out=w_bf[g][:, cols, :], in_=w_raw[g][:, :, b:N:BLOCKS].rearrange("p j m -> p m j"))
        for g in range(PASSES):
            cols = slice(g * N, (g + 1) * N)
            nc.vector.quantize_mx(
                out=w_codes[:, cols].bitcast(FP8X4), scales=w_scales[:, cols], in_=w_bf[g][:].rearrange("p m j -> p (m j)")
            )

        acc = [[psum.tile([P, HALF], F32, name=f"acc{b}_{h}") for h in range(S // HALF)] for b in range(BLOCKS)]

        codes0 = keep.tile([P, S], U32, name="x_codes0", tag="bf1", align_bytes=ALIGN)
        nc.vector.tensor_copy(codes0[:], word_table[0][:].indirect(offsets[:]))
        codes1 = keep.tile([P, S], U32, name="x_codes1", align_bytes=ALIGN)
        for h in range(S // HALF):
            entries = offsets[:, h * HALF // GROUP : (h + 1) * HALF // GROUP]
            nc.vector.tensor_copy(codes1[:, h * HALF : (h + 1) * HALF], word_table[1][:].indirect(entries))
        for b in range(BLOCKS):
            for g, codes in enumerate((codes0, codes1)):
                for h in range(S // HALF):
                    cols = slice(g * N + b * P, g * N + (b + 1) * P)
                    nc.tensor.matmul_mx(
                        out=acc[b][h][:],
                        lhsT=w_codes[:, cols].bitcast(FP8X4),
                        lhsT_scale=w_scales[:, cols],
                        rhs=codes[:, h * HALF : (h + 1) * HALF].bitcast(FP8X4),
                        rhs_scale=x_scale[:, g * S + h * HALF : g * S + (h + 1) * HALF],
                        start=(g == 0),
                        stop=(g == PASSES - 1),
                    )

        ones = keep.tile([P, 64], F32, name="ones")
        nc.vector.memset(ones[:], 1.0)

        def stretches(cuts):
            return list(zip(cuts[:-1], cuts[1:]))

        for b in range(BLOCKS):
            picked = keep.tile([P, S], F32, name=f"picked{b}")
            gate = keep.tile([P, S], F32, name=f"gate{b}")
            res = keep.tile([P, S], F32, name=f"res{b}", align_bytes=ALIGN)
            for i, (lo, hi) in enumerate(stretches(GATHER_CUTS)):
                looked_up = side_rows[b][:].indirect(offsets[:, lo // GROUP : hi // GROUP])
                if i in (0, 2):
                    nc.scalar.activation(picked[:, lo:hi], looked_up, COPY)
                elif hi == S:
                    nc.vector.tensor_tensor(picked[:, lo:hi], looked_up, ones[:], MULT)
                else:
                    nc.vector.tensor_copy(picked[:, lo:hi], looked_up)
            for lo, hi in stretches(PIECE_CUTS):
                nc.scalar.activation(gate[:, lo:hi], picked[:, lo:hi], SILU)
            for lo, hi in stretches(PIECE_CUTS):
                nc.vector.tensor_tensor(res[:, lo:hi], gate[:, lo:hi], acc[b][lo // HALF][:, lo % HALF : lo % HALF + hi - lo], MULT)
            for lo, hi in stretches(STORE_CUTS if b == BLOCKS - 1 else (0, S)):
                nc.sync.dma_start(out=out[b:N:BLOCKS, lo:hi], in_=res[:, lo:hi])
